import numpy as np
import ml_dtypes


def mxq(x, axis, fmt="e4m3"):
    dtype, down = {"e4m3": (ml_dtypes.float8_e4m3fn, 7), "e5m2": (ml_dtypes.float8_e5m2, 14)}[fmt]
    v = np.moveaxis(np.asarray(x, np.float32).astype(ml_dtypes.bfloat16).astype(np.float64), axis, -1)
    blocks = v.reshape(v.shape[:-1] + (-1, 32))
    amax = np.abs(blocks).max(-1, keepdims=True)
    byte = np.maximum(np.where(amax > 0, np.frexp(amax)[1] - 1 + 127, 0) - down, 1)
    scale = np.exp2(byte - 127.0)
    codes = (blocks / scale).astype(np.float32).astype(dtype).astype(np.float64)
    return np.moveaxis((codes * scale).reshape(v.shape), -1, axis)


WIDE = False


def mx_kscale(k):
    if not WIDE:
        return np.ones(k)
    levels = np.array([10, -10, 5, -5, 0])
    if k % 512:
        return np.exp2(np.random.permutation(np.resize(levels, k // 32))).repeat(32)
    a = np.empty((k // 512, 16))
    for p in range(k // 512):
        a[p, :8] = np.random.permutation(np.resize(levels, 8))
        for g in range(8):
            far = levels[np.abs(levels - a[p, g]) >= 10]
            a[p, g + 8] = far[np.random.randint(len(far))]
    return np.exp2(a.ravel()).repeat(32)


def f64(x):
    return np.asarray(x).astype(np.float64)


def striped(idx):
    return np.tile(idx.reshape(-1, 16).T, (8, 1)).astype(np.uint16)


def unstriped(offs):
    return offs[:16].T.reshape(-1).astype(np.int64)


E2M1 = np.array([0.0, 0.5, 1.0, 1.5, 2.0, 3.0, 4.0, 6.0, -0.0, -0.5, -1.0, -1.5, -2.0, -3.0, -4.0, -6.0])


def pack_weight(w, fmt):
    k, n = w.shape
    w = f64(np.asarray(w, np.float32).astype(ml_dtypes.bfloat16)).reshape(k // 32, 32, n)
    amax = np.abs(w).max(1)
    if fmt == "e4m3":
        byte = np.frexp(amax)[1] - 1 + 127 - 7
    else:
        mant, ex = np.frexp(amax / 6.0)
        byte = np.where(mant > 0.5, ex, ex - 1) + 127
    byte = np.clip(np.where(amax > 0, byte, 1), 1, 254)
    scaled = (w * np.exp2(127.0 - byte)[:, None, :]).reshape(k, n).astype(np.float32)
    by_word = np.ascontiguousarray(scaled.reshape(k // 512, 128, 4, n).transpose(0, 1, 3, 2))
    if fmt == "e4m3":
        words = by_word.astype(ml_dtypes.float8_e4m3fn).view(np.uint8)
    else:
        c = by_word.astype(ml_dtypes.float4_e2m1fn).view(np.uint8) & 0xF
        words = (c[..., 0::2] | (c[..., 1::2] << 4)).reshape(k // 512, 128, 2 * n)
    return np.ascontiguousarray(words), np.ascontiguousarray(byte.astype(np.uint8).reshape(k // 512, 16, n))


def unpack_weight(words, scales, fmt):
    g, _, n = scales.shape
    words = np.ascontiguousarray(words).reshape(g, 128, n, -1)
    if fmt == "e4m3":
        vals = words.view(ml_dtypes.float8_e4m3fn).astype(np.float64)
    else:
        nib = np.empty((g, 128, n, 4), np.uint8)
        nib[..., 0::2] = words & 0xF
        nib[..., 1::2] = words >> 4
        vals = E2M1[nib]
    vals = vals * np.repeat(np.exp2(scales.astype(np.float64) - 127.0), 8, axis=1)[..., None]
    return vals.transpose(0, 1, 3, 2).reshape(g * 512, n)


def gelu(v):
    return 0.5 * v * (1.0 + np.tanh(np.sqrt(2.0 / np.pi) * (v + 0.044715 * v**3)))


K, M, T, S = 1536, 1024, 4096, 1536


def setup_inputs():
    n = np.random.standard_normal
    s = mx_kscale(K)[:, None]
    u = mx_kscale(512)[:, None]
    v = pack_weight(n((K, T)) * s, "e4m3")
    p_w4 = pack_weight(n((K, M)) / np.sqrt(K) / s, "e2m1")
    return {
        "tab_words": v[0],
        "tab_scales": v[1],
        "w4_words": p_w4[0],
        "w4_scales": p_w4[1],
        "down": (n((K, 512)) / np.sqrt(K) / s * u.T).astype(np.float32),
        "up": (0.5 * n((512, M)) / np.sqrt(512) / u).astype(np.float32),
        "rT": n((M, T)).astype(np.float32),
        "b": (0.3 * n(1024)).astype(np.float32),
        "offs": striped(np.random.permutation(T)[:S]),
    }


def reference(tab_words, tab_scales, w4_words, w4_scales, down, up, rT, b, offs):
    tab_ = unpack_weight(tab_words, tab_scales, "e4m3")[:, unstriped(offs)]
    w4_ = unpack_weight(w4_words, w4_scales, "e2m1")
    down_ = mxq(f64(down), 0, "e4m3")
    up_ = mxq(f64(up), 0, "e4m3")
    h_ = mxq(down_.T @ tab_, 0, "e4m3")
    y = w4_.T @ tab_ + up_.T @ h_
    return (gelu(y + f64(b)[:, None])) + f64(rT)[:, unstriped(offs)]

@@ -1,0 +1,219 @@
+from contextlib import ExitStack
+
+import concourse.mybir as mybir
+from concourse.masks import make_identity
+
+K, M, T, S, R = 1536, 1024, 4096, 1536, 512
+FLOPS = 2 * S * (K * M + K * R + R * M)
+
+F32 = mybir.dt.float32
+BF16 = mybir.dt.bfloat16
+I32 = mybir.dt.int32
+U32 = mybir.dt.uint32
+U16 = mybir.dt.uint16
+U8 = mybir.dt.uint8
+FP8X4 = mybir.dt.float8_e4m3fn_x4
+FP4X4 = mybir.dt.float4_e2m1fn_x4
+ADD = mybir.AluOpType.add
+GELU = mybir.ActivationFunctionType.Gelu_apprx_tanh
+
+P = 128
+PACK = 4
+PASSES = K // (P * PACK)
+BANK = 512
+SLICES = S // BANK
+TILES = M // P
+QUADS = 4
+ALIGN = 64
+
+
+def tile_list_tabres_gelu_kernel(
+    tc, tab_words, tab_scales, w4_words, w4_scales, down, up, rT, b, offs, out
+):
+    nc = tc.nc
+    with ExitStack() as ctx:
+        keep = ctx.enter_context(tc.tile_pool(name="keep", bufs=1))
+        big = ctx.enter_context(tc.tile_pool(name="big", bufs=1))
+        stage = ctx.enter_context(tc.tile_pool(name="stage", bufs=4))
+        acts = ctx.enter_context(tc.tile_pool(name="acts", bufs=3))
+        psum_h = ctx.enter_context(tc.psum_pool(name="psum_h", bufs=3))
+        psum_y = ctx.enter_context(tc.psum_pool(name="psum_y", bufs=5))
+
+        def slot(n, shape, dtype, name):
+            return big.tile(shape, dtype, name=name, tag="slot%d" % n, align_bytes=ALIGN)
+
+        offsets = keep.tile([P, S // 16], U16, name="offsets")
+        nc.sync.dma_start(offsets[:], offs)
+
+        def entries(s):
+            return offsets[:, s * BANK // 16 : (s + 1) * BANK // 16]
+
+        scale_window = keep.tile([P, T], U8, name="scale_window", align_bytes=ALIGN)
+        w4_plane = keep.tile([P, PASSES, M], U8, name="w4_plane", align_bytes=ALIGN)
+        moved = keep.tile([P, PASSES - 1, S], U8, name="moved", align_bytes=ALIGN)
+        nc.vector.memset(scale_window[:].bitcast(I32), 0)
+        nc.vector.memset(w4_plane[:].bitcast(I32), 0)
+        nc.vector.memset(moved[:].bitcast(I32), 0)
+
+        b_rows = keep.tile([P, P], F32, name="b_rows")
+        nc.gpsimd.memset(b_rows[:], 0.0)
+        down_raw = []
+        for a in range(PASSES):
+            raw = slot(1 + a, [P, PACK, R], F32, "down_raw%d" % a)
+            nc.sync.dma_start(out=raw[:], in_=down[a * 512 : (a + 1) * 512, :].rearrange("(p j) r -> p j r", j=PACK))
+            down_raw.append(raw)
+            if a == 0:
+                for q in range(QUADS):
+                    nc.sync.dma_start(
+                        out=scale_window[32 * q : 32 * q + 4 * PASSES, :].bitcast(I32),
+                        in_=tab_scales[:, 4 * q : 4 * q + 4, :].bitcast(I32),
+                    )
+                nc.sync.dma_start(out=b_rows[0:TILES, :], in_=b.rearrange("(c p) -> c p", p=P))
+        table = []
+        for a in range(PASSES):
+            words = slot(4 + a, [P, T], U32, "table%d" % a)
+            nc.sync.dma_start(
+                out=words[:].bitcast(I32), in_=tab_words[a].rearrange("p t i -> p (t i)").bitcast(I32)
+            )
+            table.append(words)
+        for q in range(QUADS):
+            nc.sync.dma_start(
+                out=w4_plane[32 * q : 32 * q + 4, :, :].bitcast(I32),
+                in_=w4_scales[:, 4 * q : 4 * q + 4, :].rearrange("a r n -> r a n").bitcast(I32),
+            )
+        w4 = keep.tile([P, PASSES, 2 * M], U8, name="w4", align_bytes=ALIGN)
+        nc.sync.dma_start(out=w4[:].bitcast(I32), in_=w4_words.rearrange("a p n -> p a n").bitcast(I32))
+        up_rows = up.rearrange("(p j) n -> p j n", j=PACK)
+        up_raw0 = slot(7, [P, PACK, BANK], F32, "up_raw0")
+        nc.sync.dma_start(out=up_raw0[:], in_=up_rows[:, :, 0:BANK])
+        resid = [slot(0, [P, T], F32, "resid0")]
+        nc.sync.dma_start(out=resid[0][:], in_=rT[0:P, :])
+        up_raw1 = slot(8, [P, PACK, BANK], F32, "up_raw1")
+        nc.sync.dma_start(out=up_raw1[:], in_=up_rows[:, :, BANK : 2 * BANK])
+
+
+        ident = keep.tile([P, P], F32, name="ident")
+        make_identity(nc, ident[:])
+        b_bank = psum_h.tile([P, PACK, P], F32, name="b_bank", tag="h")
+        nc.tensor.transpose(b_bank[:, 0, :], b_rows[:], ident[:])
+        bias = keep.tile([P, TILES], F32, name="bias")
+        nc.scalar.copy(out=bias[:], in_=b_bank[:, 0, 0:TILES])
+
+        v_plane = keep.tile([P, S], U8, name="v_plane", align_bytes=ALIGN)
+        nc.vector.tensor_copy(out=v_plane[:], in_=scale_window[:].indirect(offsets[:]))
+        for a in range(1, PASSES):
+            for q in range(QUADS):
+                nc.gpsimd.dma_start(
+                    out=moved[32 * q : 32 * q + 4, a - 1, :].bitcast(I32),
+                    in_=v_plane[32 * q + 4 * a : 32 * q + 4 * a + 4, :].bitcast(I32),
+                )
+
+        down_codes = []
+        down_planes = []
+        for a in range(PASSES):
+            grouped = stage.tile([P, R * PACK], BF16, name="down_bf%d" % a, tag="grouped", align_bytes=ALIGN)
+            nc.scalar.copy(
+                out=grouped[:].rearrange("p (t m j) -> p m t j", t=PACK, j=PACK),
+                in_=down_raw[a][:].rearrange("p j (m t) -> p m t j", t=PACK),
+            )
+            codes = keep.tile([P, R], U32, name="down_codes%d" % a, align_bytes=ALIGN)
+            plane = keep.tile([P, R], U8, name="down_plane%d" % a, align_bytes=ALIGN)
+            nc.vector.quantize_mx(out=codes[:].bitcast(FP8X4), scales=plane[:], in_=grouped[:])
+            down_codes.append(codes)
+            down_planes.append(plane)
+
+        v_codes = []
+        for a in range(PASSES):
+            codes = keep.tile([P, S], U32, name="v_codes%d" % a, align_bytes=ALIGN)
+            if a < PASSES - 1:
+                nc.vector.tensor_copy(out=codes[:], in_=table[a][:].indirect(offsets[:]))
+            else:
+                for s in range(SLICES):
+                    nc.vector.tensor_copy(
+                        out=codes[:, s * BANK : (s + 1) * BANK], in_=table[a][:].indirect(entries(s))
+                    )
+            v_codes.append(codes)
+
+        up_codes = keep.tile([P, M], U32, name="up_codes", align_bytes=ALIGN)
+        up_plane = keep.tile([P, M], U8, name="up_plane", align_bytes=ALIGN)
+
+        def quantize_up(half, raw, copy):
+            grouped = stage.tile([P, BANK * PACK], BF16, name="up_bf%d" % half, tag="grouped", align_bytes=ALIGN)
+            copy(
+                out=grouped[:].rearrange("p (c i j) -> p c j i", i=4, j=PACK),
+                in_=raw[:].rearrange("p j (c i) -> p c j i", i=4),
+            )
+            cols = slice(half * BANK, (half + 1) * BANK)
+            nc.vector.quantize_mx(out=up_codes[:, cols].bitcast(FP8X4), scales=up_plane[:, cols], in_=grouped[:])
+
+        quantize_up(0, up_raw0, nc.vector.tensor_copy)
+
+        h_codes = keep.tile([P, S], U32, name="h_codes", align_bytes=ALIGN)
+        h_plane = keep.tile([P, S], U8, name="h_plane", align_bytes=ALIGN)
+        for s in range(SLICES):
+            grouped = stage.tile([P, BANK * PACK], BF16, name="h_bf%d" % s, tag="grouped", align_bytes=ALIGN)
+            for c in range(BANK // P):
+                cols = slice(s * BANK + c * P, s * BANK + (c + 1) * P)
+                bank = psum_h.tile([P, PACK, P], F32, name="h_bank", tag="h")
+                for t in range(PACK):
+                    for a in range(PASSES):
+                        nc.tensor.matmul_mx(
+                            out=bank[:, t, :],
+                            lhsT=down_codes[a][:, t * P : (t + 1) * P].bitcast(FP8X4),
+                            lhsT_scale=down_planes[a][:, t * P : (t + 1) * P],
+                            rhs=v_codes[a][:, cols].bitcast(FP8X4),
+                            rhs_scale=v_plane[4 * a : P, cols],
+                            start=(a == 0),
+                            stop=(a == PASSES - 1),
+                        )
+                nc.scalar.copy(
+                    out=grouped[:, c * P * PACK : (c + 1) * P * PACK].rearrange("p (n t) -> p n t", t=PACK),
+                    in_=bank[:].rearrange("p t n -> p n t"),
+                )
+            cols = slice(s * BANK, (s + 1) * BANK)
+            nc.vector.quantize_mx(out=h_codes[:, cols].bitcast(FP8X4), scales=h_plane[:, cols], in_=grouped[:])
+
+        for i in range(1, TILES):
+            rows = slot(i, [P, T], F32, "resid%d" % i)
+            nc.sync.dma_start(out=rows[:], in_=rT[i * P : (i + 1) * P, :])
+            resid.append(rows)
+
+        quantize_up(1, up_raw1, nc.scalar.copy)
+
+        for i in range(TILES):
+            act = acts.tile([P, S], F32, name="act")
+            result = slot(i - 1 if i > 0 else 9, [P, S], F32, "result%d" % i)
+            by_slice = i in (0, TILES - 1)
+            for s in range(SLICES):
+                cols = slice(s * BANK, (s + 1) * BANK)
+                bank = psum_y.tile([P, BANK], F32, name="y_bank")
+                for a in range(PASSES):
+                    nc.tensor.matmul_mx(
+                        out=bank[:],
+                        lhsT=w4[:, a, 2 * i * P : 2 * (i + 1) * P].bitcast(FP4X4),
+                        lhsT_scale=w4_plane[:, a, i * P : (i + 1) * P],
+                        rhs=v_codes[a][:, cols].bitcast(FP8X4),
+                        rhs_scale=v_plane[:, cols] if a == 0 else moved[:, a - 1, cols],
+                        start=(a == 0),
+                        stop=False,
+                    )
+                nc.tensor.matmul_mx(
+                    out=bank[:],
+                    lhsT=up_codes[:, i * P : (i + 1) * P].bitcast(FP8X4),
+                    lhsT_scale=up_plane[:, i * P : (i + 1) * P],
+                    rhs=h_codes[:, cols].bitcast(FP8X4),
+                    rhs_scale=h_plane[:, cols],
+                    start=False,
+                    stop=True,
+                )
+                nc.scalar.activation(out=act[:, cols], in_=bank[:], func=GELU, bias=bias[:, i : i + 1])
+                if by_slice:
+                    nc.vector.tensor_tensor(
+                        out=result[:, cols], in0=resid[i][:].indirect(entries(s)), in1=act[:, cols], op=ADD
+                    )
+                if i == TILES - 1:
+                    nc.sync.dma_start(out=out[i * P : (i + 1) * P, cols], in_=result[:, cols])
+            if not by_slice:
+                nc.vector.tensor_tensor(out=result[:], in0=resid[i][:].indirect(offsets[:]), in1=act[:], op=ADD)
+            if i < TILES - 1:
+                nc.sync.dma_start(out=out[i * P : (i + 1) * P, :], in_=result[:])

@@ -25,6 +25,9 @@ SLICES = S // BANK
 TILES = M // P
 QUADS = 4
 ALIGN = 64
+WIDE = 2
+LIVE = 100
+UP_AFTER = 2
 
 
 def tile_list_tabres_gelu_kernel(
@@ -34,10 +37,9 @@ def tile_list_tabres_gelu_kernel(
     with ExitStack() as ctx:
         keep = ctx.enter_context(tc.tile_pool(name="keep", bufs=1))
         big = ctx.enter_context(tc.tile_pool(name="big", bufs=1))
-        stage = ctx.enter_context(tc.tile_pool(name="stage", bufs=4))
+        stage = ctx.enter_context(tc.tile_pool(name="stage", bufs=5))
         acts = ctx.enter_context(tc.tile_pool(name="acts", bufs=3))
-        psum_h = ctx.enter_context(tc.psum_pool(name="psum_h", bufs=3))
-        psum_y = ctx.enter_context(tc.psum_pool(name="psum_y", bufs=5))
+        psum = ctx.enter_context(tc.psum_pool(name="psum", bufs=8))
 
         def slot(n, shape, dtype, name):
             return big.tile(shape, dtype, name=name, tag="slot%d" % n, align_bytes=ALIGN)
@@ -55,8 +57,6 @@ def tile_list_tabres_gelu_kernel(
         nc.vector.memset(w4_plane[:].bitcast(I32), 0)
         nc.vector.memset(moved[:].bitcast(I32), 0)
 
-        b_rows = keep.tile([P, P], F32, name="b_rows")
-        nc.gpsimd.memset(b_rows[:], 0.0)
         down_raw = []
         for a in range(PASSES):
             raw = slot(1 + a, [P, PACK, R], F32, "down_raw%d" % a)
@@ -68,7 +68,6 @@ def tile_list_tabres_gelu_kernel(
                         out=scale_window[32 * q : 32 * q + 4 * PASSES, :].bitcast(I32),
                         in_=tab_scales[:, 4 * q : 4 * q + 4, :].bitcast(I32),
                     )
-                nc.sync.dma_start(out=b_rows[0:TILES, :], in_=b.rearrange("(c p) -> c p", p=P))
         table = []
         for a in range(PASSES):
             words = slot(4 + a, [P, T], U32, "table%d" % a)
@@ -81,6 +80,9 @@ def tile_list_tabres_gelu_kernel(
                 out=w4_plane[32 * q : 32 * q + 4, :, :].bitcast(I32),
                 in_=w4_scales[:, 4 * q : 4 * q + 4, :].rearrange("a r n -> r a n").bitcast(I32),
             )
+        b_rows = keep.tile([P, P], F32, name="b_rows")
+        nc.gpsimd.memset(b_rows[:], 0.0)
+        nc.gpsimd.dma_start(out=b_rows[0:TILES, :], in_=b.rearrange("(c p) -> c p", p=P))
         w4 = keep.tile([P, PASSES, 2 * M], U8, name="w4", align_bytes=ALIGN)
         nc.sync.dma_start(out=w4[:].bitcast(I32), in_=w4_words.rearrange("a p n -> p a n").bitcast(I32))
         up_rows = up.rearrange("(p j) n -> p j n", j=PACK)
@@ -88,25 +90,21 @@ def tile_list_tabres_gelu_kernel(
         nc.sync.dma_start(out=up_raw0[:], in_=up_rows[:, :, 0:BANK])
         resid = [slot(0, [P, T], F32, "resid0")]
         nc.sync.dma_start(out=resid[0][:], in_=rT[0:P, :])
-        up_raw1 = slot(8, [P, PACK, BANK], F32, "up_raw1")
-        nc.sync.dma_start(out=up_raw1[:], in_=up_rows[:, :, BANK : 2 * BANK])
 
 
         ident = keep.tile([P, P], F32, name="ident")
         make_identity(nc, ident[:])
-        b_bank = psum_h.tile([P, PACK, P], F32, name="b_bank", tag="h")
-        nc.tensor.transpose(b_bank[:, 0, :], b_rows[:], ident[:])
+        b_bank = psum.tile([P, BANK], F32, name="b_bank", tag="bank")
+        nc.tensor.transpose(b_bank[:, 0:P], b_rows[:], ident[:])
         bias = keep.tile([P, TILES], F32, name="bias")
-        nc.scalar.copy(out=bias[:], in_=b_bank[:, 0, 0:TILES])
+        nc.scalar.copy(out=bias[:], in_=b_bank[:, 0:TILES])
 
         v_plane = keep.tile([P, S], U8, name="v_plane", align_bytes=ALIGN)
         nc.vector.tensor_copy(out=v_plane[:], in_=scale_window[:].indirect(offsets[:]))
         for a in range(1, PASSES):
-            for q in range(QUADS):
-                nc.gpsimd.dma_start(
-                    out=moved[32 * q : 32 * q + 4, a - 1, :].bitcast(I32),
-                    in_=v_plane[32 * q + 4 * a : 32 * q + 4 * a + 4, :].bitcast(I32),
-                )
+            nc.gpsimd.dma_start(
+                out=moved[0:LIVE, a - 1, :].bitcast(I32), in_=v_plane[4 * a : 4 * a + LIVE, :].bitcast(I32)
+            )
 
         down_codes = []
         down_planes = []
@@ -124,15 +122,32 @@ def tile_list_tabres_gelu_kernel(
 
         v_codes = []
         for a in range(PASSES):
-            codes = keep.tile([P, S], U32, name="v_codes%d" % a, align_bytes=ALIGN)
-            if a < PASSES - 1:
-                nc.vector.tensor_copy(out=codes[:], in_=table[a][:].indirect(offsets[:]))
-            else:
-                for s in range(SLICES):
-                    nc.vector.tensor_copy(
-                        out=codes[:, s * BANK : (s + 1) * BANK], in_=table[a][:].indirect(entries(s))
-                    )
-            v_codes.append(codes)
+            v_codes.append(keep.tile([P, S], U32, name="v_codes%d" % a, align_bytes=ALIGN))
+
+        def h_pass(bank, t, a, cols):
+            nc.tensor.matmul_mx(
+                out=bank,
+                lhsT=down_codes[a][:, t * P : (t + 1) * P].bitcast(FP8X4),
+                lhsT_scale=down_planes[a][:, t * P : (t + 1) * P],
+                rhs=v_codes[a][:, cols].bitcast(FP8X4),
+                rhs_scale=v_plane[4 * a : P, cols],
+                start=(a == 0),
+                stop=(a == PASSES - 1),
+            )
+
+        wide = []
+        for s in range(WIDE):
+            wide.append([psum.tile([P, BANK], F32, name="h_wide%d_%d" % (s, t), tag="bank") for t in range(PACK)])
+        for a in range(PASSES - 1):
+            nc.vector.tensor_copy(out=v_codes[a][:], in_=table[a][:].indirect(offsets[:]))
+            for s in range(WIDE):
+                for t in range(PACK):
+                    h_pass(wide[s][t][:], t, a, slice(s * BANK, (s + 1) * BANK))
+        last = PASSES - 1
+        for s in range(SLICES):
+            nc.vector.tensor_copy(
+                out=v_codes[last][:, s * BANK : (s + 1) * BANK], in_=table[last][:].indirect(entries(s))
+            )
 
         up_codes = keep.tile([P, M], U32, name="up_codes", align_bytes=ALIGN)
         up_plane = keep.tile([P, M], U8, name="up_plane", align_bytes=ALIGN)
@@ -146,39 +161,46 @@ def tile_list_tabres_gelu_kernel(
             cols = slice(half * BANK, (half + 1) * BANK)
             nc.vector.quantize_mx(out=up_codes[:, cols].bitcast(FP8X4), scales=up_plane[:, cols], in_=grouped[:])
 
-        quantize_up(0, up_raw0, nc.vector.tensor_copy)
-
-        h_codes = keep.tile([P, S], U32, name="h_codes", align_bytes=ALIGN)
-        h_plane = keep.tile([P, S], U8, name="h_plane", align_bytes=ALIGN)
-        for s in range(SLICES):
-            grouped = stage.tile([P, BANK * PACK], BF16, name="h_bf%d" % s, tag="grouped", align_bytes=ALIGN)
-            for c in range(BANK // P):
-                cols = slice(s * BANK + c * P, s * BANK + (c + 1) * P)
-                bank = psum_h.tile([P, PACK, P], F32, name="h_bank", tag="h")
-                for t in range(PACK):
-                    for a in range(PASSES):
-                        nc.tensor.matmul_mx(
-                            out=bank[:, t, :],
-                            lhsT=down_codes[a][:, t * P : (t + 1) * P].bitcast(FP8X4),
-                            lhsT_scale=down_planes[a][:, t * P : (t + 1) * P],
-                            rhs=v_codes[a][:, cols].bitcast(FP8X4),
-                            rhs_scale=v_plane[4 * a : P, cols],
-                            start=(a == 0),
-                            stop=(a == PASSES - 1),
-                        )
-                nc.scalar.copy(
-                    out=grouped[:, c * P * PACK : (c + 1) * P * PACK].rearrange("p (n t) -> p n t", t=PACK),
-                    in_=bank[:].rearrange("p t n -> p n t"),
-                )
-            cols = slice(s * BANK, (s + 1) * BANK)
-            nc.vector.quantize_mx(out=h_codes[:, cols].bitcast(FP8X4), scales=h_plane[:, cols], in_=grouped[:])
-
-        for i in range(1, TILES):
+        def load_resid(i):
             rows = slot(i, [P, T], F32, "resid%d" % i)
             nc.sync.dma_start(out=rows[:], in_=rT[i * P : (i + 1) * P, :])
             resid.append(rows)
 
-        quantize_up(1, up_raw1, nc.scalar.copy)
+        for i in range(1, UP_AFTER):
+            load_resid(i)
+        up_raw1 = slot(8, [P, PACK, BANK], F32, "up_raw1")
+        nc.sync.dma_start(out=up_raw1[:], in_=up_rows[:, :, BANK : 2 * BANK])
+        for i in range(UP_AFTER, TILES - 1):
+            load_resid(i)
+
+        h_codes = keep.tile([P, S], U32, name="h_codes", align_bytes=ALIGN)
+        h_plane = keep.tile([P, S], U8, name="h_plane", align_bytes=ALIGN)
+        for s in range(SLICES):
+            cols = slice(s * BANK, (s + 1) * BANK)
+            grouped = stage.tile([P, BANK * PACK], BF16, name="h_bf%d" % s, tag="grouped", align_bytes=ALIGN)
+            if s < WIDE:
+                apart = stage.tile([P, PACK, BANK], BF16, name="h_apart%d" % s, tag="grouped", align_bytes=ALIGN)
+                for t in range(PACK):
+                    h_pass(wide[s][t][:], t, last, cols)
+                    nc.scalar.copy(out=apart[:, t, :], in_=wide[s][t][:])
+                nc.vector.tensor_copy(
+                    out=grouped[:].rearrange("p (c i t) -> p c t i", i=4, t=PACK),
+                    in_=apart[:].rearrange("p t (c i) -> p c t i", i=4),
+                )
+            else:
+                for c in range(BANK // P):
+                    bank = psum.tile([P, PACK, P], F32, name="h_bank", tag="bank")
+                    for t in range(PACK):
+                        for a in range(PASSES):
+                            h_pass(bank[:, t, :], t, a, slice(s * BANK + c * P, s * BANK + (c + 1) * P))
+                    nc.scalar.copy(
+                        out=grouped[:, c * P * PACK : (c + 1) * P * PACK].rearrange("p (n t) -> p n t", t=PACK),
+                        in_=bank[:].rearrange("p t n -> p n t"),
+                    )
+            nc.vector.quantize_mx(out=h_codes[:, cols].bitcast(FP8X4), scales=h_plane[:, cols], in_=grouped[:])
+            if s == 0:
+                quantize_up(0, up_raw0, nc.vector.tensor_copy)
+        load_resid(TILES - 1)
 
         for i in range(TILES):
             act = acts.tile([P, S], F32, name="act")
@@ -186,7 +208,7 @@ def tile_list_tabres_gelu_kernel(
             by_slice = i in (0, TILES - 1)
             for s in range(SLICES):
                 cols = slice(s * BANK, (s + 1) * BANK)
-                bank = psum_y.tile([P, BANK], F32, name="y_bank")
+                bank = psum.tile([P, BANK], F32, name="y_bank", tag="bank")
                 for a in range(PASSES):
                     nc.tensor.matmul_mx(
                         out=bank[:],
@@ -215,5 +237,7 @@ def tile_list_tabres_gelu_kernel(
                     nc.sync.dma_start(out=out[i * P : (i + 1) * P, cols], in_=result[:, cols])
             if not by_slice:
                 nc.vector.tensor_tensor(out=result[:], in0=resid[i][:].indirect(offsets[:]), in1=act[:], op=ADD)
+            if i == 1:
+                quantize_up(1, up_raw1, nc.scalar.copy)
             if i < TILES - 1:
                 nc.sync.dma_start(out=out[i * P : (i + 1) * P, :], in_=result[:])

@@ -64,10 +64,13 @@ def tile_list_tabres_gelu_kernel(
             down_raw.append(raw)
             if a == 0:
                 for q in range(QUADS):
-                    nc.sync.dma_start(
+                    nc.gpsimd.dma_start(
                         out=scale_window[32 * q : 32 * q + 4 * PASSES, :].bitcast(I32),
                         in_=tab_scales[:, 4 * q : 4 * q + 4, :].bitcast(I32),
                     )
+        b_rows = keep.tile([P, P], F32, name="b_rows")
+        nc.gpsimd.memset(b_rows[:], 0.0)
+        nc.gpsimd.dma_start(out=b_rows[0:TILES, :], in_=b.rearrange("(c p) -> c p", p=P))
         table = []
         for a in range(PASSES):
             words = slot(4 + a, [P, T], U32, "table%d" % a)
@@ -76,13 +79,10 @@ def tile_list_tabres_gelu_kernel(
             )
             table.append(words)
         for q in range(QUADS):
-            nc.sync.dma_start(
+            nc.gpsimd.dma_start(
                 out=w4_plane[32 * q : 32 * q + 4, :, :].bitcast(I32),
                 in_=w4_scales[:, 4 * q : 4 * q + 4, :].rearrange("a r n -> r a n").bitcast(I32),
             )
-        b_rows = keep.tile([P, P], F32, name="b_rows")
-        nc.gpsimd.memset(b_rows[:], 0.0)
-        nc.gpsimd.dma_start(out=b_rows[0:TILES, :], in_=b.rearrange("(c p) -> c p", p=P))
         w4 = keep.tile([P, PASSES, 2 * M], U8, name="w4", align_bytes=ALIGN)
         nc.sync.dma_start(out=w4[:].bitcast(I32), in_=w4_words.rearrange("a p n -> p a n").bitcast(I32))
         up_rows = up.rearrange("(p j) n -> p j n", j=PACK)

@@ -26,7 +26,7 @@ TILES = M // P
 QUADS = 4
 ALIGN = 64
 WIDE = 2
-LIVE = 100
+EARLY = 4
 UP_AFTER = 2
 
 
@@ -45,7 +45,6 @@ def tile_list_tabres_gelu_kernel(
             return big.tile(shape, dtype, name=name, tag="slot%d" % n, align_bytes=ALIGN)
 
         offsets = keep.tile([P, S // 16], U16, name="offsets")
-        nc.sync.dma_start(offsets[:], offs)
 
         def entries(s):
             return offsets[:, s * BANK // 16 : (s + 1) * BANK // 16]
@@ -63,6 +62,7 @@ def tile_list_tabres_gelu_kernel(
             nc.sync.dma_start(out=raw[:], in_=down[a * 512 : (a + 1) * 512, :].rearrange("(p j) r -> p j r", j=PACK))
             down_raw.append(raw)
             if a == 0:
+                nc.sync.dma_start(offsets[:], offs)
                 for q in range(QUADS):
                     nc.gpsimd.dma_start(
                         out=scale_window[32 * q : 32 * q + 4 * PASSES, :].bitcast(I32),
@@ -102,9 +102,11 @@ def tile_list_tabres_gelu_kernel(
         v_plane = keep.tile([P, S], U8, name="v_plane", align_bytes=ALIGN)
         nc.vector.tensor_copy(out=v_plane[:], in_=scale_window[:].indirect(offsets[:]))
         for a in range(1, PASSES):
-            nc.gpsimd.dma_start(
-                out=moved[0:LIVE, a - 1, :].bitcast(I32), in_=v_plane[4 * a : 4 * a + LIVE, :].bitcast(I32)
-            )
+            for q in range(QUADS):
+                nc.gpsimd.dma_start(
+                    out=moved[32 * q : 32 * q + 4, a - 1, :].bitcast(I32),
+                    in_=v_plane[32 * q + 4 * a : 32 * q + 4 * a + 4, :].bitcast(I32),
+                )
 
         down_codes = []
         down_planes = []
@@ -205,7 +207,9 @@ def tile_list_tabres_gelu_kernel(
         for i in range(TILES):
             act = acts.tile([P, S], F32, name="act")
             result = slot(i - 1 if i > 0 else 9, [P, S], F32, "result%d" % i)
-            by_slice = i in (0, TILES - 1)
+            by_slice = i == TILES - 1
+            if i < EARLY:
+                nc.vector.tensor_copy(out=result[:], in_=resid[i][:].indirect(offsets[:]))
             for s in range(SLICES):
                 cols = slice(s * BANK, (s + 1) * BANK)
                 bank = psum.tile([P, BANK], F32, name="y_bank", tag="bank")
@@ -235,7 +239,9 @@ def tile_list_tabres_gelu_kernel(
                     )
                 if i == TILES - 1:
                     nc.sync.dma_start(out=out[i * P : (i + 1) * P, cols], in_=result[:, cols])
-            if not by_slice:
+            if i < EARLY:
+                nc.vector.tensor_tensor(out=result[:], in0=result[:], in1=act[:], op=ADD)
+            elif not by_slice:
                 nc.vector.tensor_tensor(out=result[:], in0=resid[i][:].indirect(offsets[:]), in1=act[:], op=ADD)
             if i == 1:
                 quantize_up(1, up_raw1, nc.scalar.copy)

@@ -19,15 +19,21 @@ GELU = mybir.ActivationFunctionType.Gelu_apprx_tanh
 
 P = 128
 PACK = 4
-PASSES = K // (P * PACK)
+K_PASS = P * PACK
+PASSES = K // K_PASS
 BANK = 512
+BANKS = 8
 SLICES = S // BANK
 TILES = M // P
 QUADS = 4
+QUAD = P // QUADS
+PLANE_ROWS = 4
+GROUP = 16
+LINE = 4
 ALIGN = 64
-WIDE = 2
-EARLY = 4
-UP_AFTER = 2
+EARLY_SLICES = BANKS // PACK
+STAGE_BUFS = 6
+ACT_BUFS = 3
 
 
 def tile_list_tabres_gelu_kernel(
@@ -37,17 +43,20 @@ def tile_list_tabres_gelu_kernel(
     with ExitStack() as ctx:
         keep = ctx.enter_context(tc.tile_pool(name="keep", bufs=1))
         big = ctx.enter_context(tc.tile_pool(name="big", bufs=1))
-        stage = ctx.enter_context(tc.tile_pool(name="stage", bufs=5))
-        acts = ctx.enter_context(tc.tile_pool(name="acts", bufs=3))
-        psum = ctx.enter_context(tc.psum_pool(name="psum", bufs=8))
+        stage = ctx.enter_context(tc.tile_pool(name="stage", bufs=STAGE_BUFS))
+        acts = ctx.enter_context(tc.tile_pool(name="acts", bufs=ACT_BUFS))
+        psum = ctx.enter_context(tc.psum_pool(name="psum", bufs=BANKS))
 
         def slot(n, shape, dtype, name):
             return big.tile(shape, dtype, name=name, tag="slot%d" % n, align_bytes=ALIGN)
 
-        offsets = keep.tile([P, S // 16], U16, name="offsets")
+        def token_cols(s):
+            return slice(s * BANK, (s + 1) * BANK)
+
+        offsets = keep.tile([P, S // GROUP], U16, name="offsets")
 
         def entries(s):
-            return offsets[:, s * BANK // 16 : (s + 1) * BANK // 16]
+            return offsets[:, s * BANK // GROUP : (s + 1) * BANK // GROUP]
 
         scale_window = keep.tile([P, T], U8, name="scale_window", align_bytes=ALIGN)
         w4_plane = keep.tile([P, PASSES, M], U8, name="w4_plane", align_bytes=ALIGN)
@@ -59,38 +68,44 @@ def tile_list_tabres_gelu_kernel(
         down_raw = []
         for a in range(PASSES):
             raw = slot(1 + a, [P, PACK, R], F32, "down_raw%d" % a)
-            nc.sync.dma_start(out=raw[:], in_=down[a * 512 : (a + 1) * 512, :].rearrange("(p j) r -> p j r", j=PACK))
+            nc.sync.dma_start(
+                out=raw[:], in_=down[a * K_PASS : (a + 1) * K_PASS, :].rearrange("(p j) r -> p j r", j=PACK)
+            )
             down_raw.append(raw)
             if a == 0:
                 nc.sync.dma_start(offsets[:], offs)
                 for q in range(QUADS):
                     nc.gpsimd.dma_start(
-                        out=scale_window[32 * q : 32 * q + 4 * PASSES, :].bitcast(I32),
-                        in_=tab_scales[:, 4 * q : 4 * q + 4, :].bitcast(I32),
+                        out=scale_window[QUAD * q : QUAD * q + PLANE_ROWS * PASSES, :].bitcast(I32),
+                        in_=tab_scales[:, PLANE_ROWS * q : PLANE_ROWS * (q + 1), :].bitcast(I32),
                     )
         b_rows = keep.tile([P, P], F32, name="b_rows")
         nc.gpsimd.memset(b_rows[:], 0.0)
         nc.gpsimd.dma_start(out=b_rows[0:TILES, :], in_=b.rearrange("(c p) -> c p", p=P))
         table = []
         for a in range(PASSES):
-            words = slot(4 + a, [P, T], U32, "table%d" % a)
+            words = slot(1 + PASSES + a, [P, T], U32, "table%d" % a)
             nc.sync.dma_start(
                 out=words[:].bitcast(I32), in_=tab_words[a].rearrange("p t i -> p (t i)").bitcast(I32)
             )
             table.append(words)
         for q in range(QUADS):
             nc.gpsimd.dma_start(
-                out=w4_plane[32 * q : 32 * q + 4, :, :].bitcast(I32),
-                in_=w4_scales[:, 4 * q : 4 * q + 4, :].rearrange("a r n -> r a n").bitcast(I32),
+                out=w4_plane[QUAD * q : QUAD * q + PLANE_ROWS, :, :].bitcast(I32),
+                in_=w4_scales[:, PLANE_ROWS * q : PLANE_ROWS * (q + 1), :].rearrange("a r n -> r a n").bitcast(I32),
             )
         w4 = keep.tile([P, PASSES, 2 * M], U8, name="w4", align_bytes=ALIGN)
         nc.sync.dma_start(out=w4[:].bitcast(I32), in_=w4_words.rearrange("a p n -> p a n").bitcast(I32))
-        up_rows = up.rearrange("(p j) n -> p j n", j=PACK)
-        up_raw0 = slot(7, [P, PACK, BANK], F32, "up_raw0")
-        nc.sync.dma_start(out=up_raw0[:], in_=up_rows[:, :, 0:BANK])
-        resid = [slot(0, [P, T], F32, "resid0")]
-        nc.sync.dma_start(out=resid[0][:], in_=rT[0:P, :])
+        up_raw = slot(TILES - 1, [P, PACK, M], F32, "up_raw")
+        nc.sync.dma_start(out=up_raw[:], in_=up.rearrange("(p j) n -> p j n", j=PACK))
+        resid = []
 
+        def load_resid(i):
+            rows = slot(i, [P, T], F32, "resid%d" % i)
+            nc.sync.dma_start(out=rows[:], in_=rT[i * P : (i + 1) * P, :])
+            resid.append(rows)
+
+        load_resid(0)
 
         ident = keep.tile([P, P], F32, name="ident")
         make_identity(nc, ident[:])
@@ -103,9 +118,10 @@ def tile_list_tabres_gelu_kernel(
         nc.vector.tensor_copy(out=v_plane[:], in_=scale_window[:].indirect(offsets[:]))
         for a in range(1, PASSES):
             for q in range(QUADS):
+                first = QUAD * q + PLANE_ROWS * a
                 nc.gpsimd.dma_start(
-                    out=moved[32 * q : 32 * q + 4, a - 1, :].bitcast(I32),
-                    in_=v_plane[32 * q + 4 * a : 32 * q + 4 * a + 4, :].bitcast(I32),
+                    out=moved[QUAD * q : QUAD * q + PLANE_ROWS, a - 1, :].bitcast(I32),
+                    in_=v_plane[first : first + PLANE_ROWS, :].bitcast(I32),
                 )
 
         down_codes = []
@@ -126,98 +142,86 @@ def tile_list_tabres_gelu_kernel(
         for a in range(PASSES):
             v_codes.append(keep.tile([P, S], U32, name="v_codes%d" % a, align_bytes=ALIGN))
 
-        def h_pass(bank, t, a, cols):
+        def h_pass(sums, t, a, cols):
             nc.tensor.matmul_mx(
-                out=bank,
+                out=sums,
                 lhsT=down_codes[a][:, t * P : (t + 1) * P].bitcast(FP8X4),
                 lhsT_scale=down_planes[a][:, t * P : (t + 1) * P],
                 rhs=v_codes[a][:, cols].bitcast(FP8X4),
-                rhs_scale=v_plane[4 * a : P, cols],
+                rhs_scale=v_plane[PLANE_ROWS * a : P, cols],
                 start=(a == 0),
                 stop=(a == PASSES - 1),
             )
 
-        wide = []
-        for s in range(WIDE):
-            wide.append([psum.tile([P, BANK], F32, name="h_wide%d_%d" % (s, t), tag="bank") for t in range(PACK)])
-        for a in range(PASSES - 1):
-            nc.vector.tensor_copy(out=v_codes[a][:], in_=table[a][:].indirect(offsets[:]))
-            for s in range(WIDE):
-                for t in range(PACK):
-                    h_pass(wide[s][t][:], t, a, slice(s * BANK, (s + 1) * BANK))
         last = PASSES - 1
+        early = []
+        for s in range(EARLY_SLICES):
+            early.append([psum.tile([P, BANK], F32, name="h_early%d_%d" % (s, t), tag="bank") for t in range(PACK)])
+        for a in range(last):
+            nc.vector.tensor_copy(out=v_codes[a][:], in_=table[a][:].indirect(offsets[:]))
+            for s in range(EARLY_SLICES):
+                for t in range(PACK):
+                    h_pass(early[s][t][:], t, a, token_cols(s))
         for s in range(SLICES):
-            nc.vector.tensor_copy(
-                out=v_codes[last][:, s * BANK : (s + 1) * BANK], in_=table[last][:].indirect(entries(s))
-            )
+            nc.vector.tensor_copy(out=v_codes[last][:, token_cols(s)], in_=table[last][:].indirect(entries(s)))
 
         up_codes = keep.tile([P, M], U32, name="up_codes", align_bytes=ALIGN)
         up_plane = keep.tile([P, M], U8, name="up_plane", align_bytes=ALIGN)
 
-        def quantize_up(half, raw, copy):
-            grouped = stage.tile([P, BANK * PACK], BF16, name="up_bf%d" % half, tag="grouped", align_bytes=ALIGN)
+        def quantize_up(half, copy):
+            cols = slice(half * M // 2, (half + 1) * M // 2)
+            grouped = stage.tile([P, M // 2 * PACK], BF16, name="up_bf%d" % half, tag="grouped", align_bytes=ALIGN)
             copy(
-                out=grouped[:].rearrange("p (c i j) -> p c j i", i=4, j=PACK),
-                in_=raw[:].rearrange("p j (c i) -> p c j i", i=4),
+                out=grouped[:].rearrange("p (c i j) -> p c j i", i=LINE, j=PACK),
+                in_=up_raw[:, :, cols].rearrange("p j (c i) -> p c j i", i=LINE),
             )
-            cols = slice(half * BANK, (half + 1) * BANK)
             nc.vector.quantize_mx(out=up_codes[:, cols].bitcast(FP8X4), scales=up_plane[:, cols], in_=grouped[:])
 
-        def load_resid(i):
-            rows = slot(i, [P, T], F32, "resid%d" % i)
-            nc.sync.dma_start(out=rows[:], in_=rT[i * P : (i + 1) * P, :])
-            resid.append(rows)
-
-        for i in range(1, UP_AFTER):
-            load_resid(i)
-        up_raw1 = slot(8, [P, PACK, BANK], F32, "up_raw1")
-        nc.sync.dma_start(out=up_raw1[:], in_=up_rows[:, :, BANK : 2 * BANK])
-        for i in range(UP_AFTER, TILES - 1):
+        for i in range(1, TILES - 1):
             load_resid(i)
 
         h_codes = keep.tile([P, S], U32, name="h_codes", align_bytes=ALIGN)
         h_plane = keep.tile([P, S], U8, name="h_plane", align_bytes=ALIGN)
         for s in range(SLICES):
-            cols = slice(s * BANK, (s + 1) * BANK)
+            cols = token_cols(s)
             grouped = stage.tile([P, BANK * PACK], BF16, name="h_bf%d" % s, tag="grouped", align_bytes=ALIGN)
-            if s < WIDE:
+            if s < EARLY_SLICES:
                 apart = stage.tile([P, PACK, BANK], BF16, name="h_apart%d" % s, tag="grouped", align_bytes=ALIGN)
                 for t in range(PACK):
-                    h_pass(wide[s][t][:], t, last, cols)
-                    nc.scalar.copy(out=apart[:, t, :], in_=wide[s][t][:])
+                    h_pass(early[s][t][:], t, last, cols)
+                    nc.scalar.copy(out=apart[:, t, :], in_=early[s][t][:])
                 nc.vector.tensor_copy(
-                    out=grouped[:].rearrange("p (c i t) -> p c t i", i=4, t=PACK),
-                    in_=apart[:].rearrange("p t (c i) -> p c t i", i=4),
+                    out=grouped[:].rearrange("p (c i t) -> p c t i", i=LINE, t=PACK),
+                    in_=apart[:].rearrange("p t (c i) -> p c t i", i=LINE),
                 )
             else:
                 for c in range(BANK // P):
-                    bank = psum.tile([P, PACK, P], F32, name="h_bank", tag="bank")
+                    shared = psum.tile([P, PACK, P], F32, name="h_shared", tag="bank")
                     for t in range(PACK):
                         for a in range(PASSES):
-                            h_pass(bank[:, t, :], t, a, slice(s * BANK + c * P, s * BANK + (c + 1) * P))
+                            h_pass(shared[:, t, :], t, a, slice(s * BANK + c * P, s * BANK + (c + 1) * P))
                     nc.scalar.copy(
                         out=grouped[:, c * P * PACK : (c + 1) * P * PACK].rearrange("p (n t) -> p n t", t=PACK),
-                        in_=bank[:].rearrange("p t n -> p n t"),
+                        in_=shared[:].rearrange("p t n -> p n t"),
                     )
             nc.vector.quantize_mx(out=h_codes[:, cols].bitcast(FP8X4), scales=h_plane[:, cols], in_=grouped[:])
             if s == 0:
-                quantize_up(0, up_raw0, nc.vector.tensor_copy)
+                quantize_up(0, nc.vector.tensor_copy)
+        quantize_up(1, nc.scalar.copy)
         load_resid(TILES - 1)
 
         for i in range(TILES):
+            rows = slice(i * P, (i + 1) * P)
             act = acts.tile([P, S], F32, name="act")
-            result = slot(i - 1 if i > 0 else 9, [P, S], F32, "result%d" % i)
-            by_slice = i == TILES - 1
-            if i < EARLY:
-                nc.vector.tensor_copy(out=result[:], in_=resid[i][:].indirect(offsets[:]))
+            result = slot(i - 1 if i > 0 else TILES, [P, S], F32, "result%d" % i)
             for s in range(SLICES):
-                cols = slice(s * BANK, (s + 1) * BANK)
+                cols = token_cols(s)
                 bank = psum.tile([P, BANK], F32, name="y_bank", tag="bank")
                 for a in range(PASSES):
                     nc.tensor.matmul_mx(
                         out=bank[:],
                         lhsT=w4[:, a, 2 * i * P : 2 * (i + 1) * P].bitcast(FP4X4),
-                        lhsT_scale=w4_plane[:, a, i * P : (i + 1) * P],
+                        lhsT_scale=w4_plane[:, a, rows],
                         rhs=v_codes[a][:, cols].bitcast(FP8X4),
                         rhs_scale=v_plane[:, cols] if a == 0 else moved[:, a - 1, cols],
                         start=(a == 0),
@@ -225,25 +229,18 @@ def tile_list_tabres_gelu_kernel(
                     )
                 nc.tensor.matmul_mx(
                     out=bank[:],
-                    lhsT=up_codes[:, i * P : (i + 1) * P].bitcast(FP8X4),
-                    lhsT_scale=up_plane[:, i * P : (i + 1) * P],
+                    lhsT=up_codes[:, rows].bitcast(FP8X4),
+                    lhsT_scale=up_plane[:, rows],
                     rhs=h_codes[:, cols].bitcast(FP8X4),
                     rhs_scale=h_plane[:, cols],
                     start=False,
                     stop=True,
                 )
                 nc.scalar.activation(out=act[:, cols], in_=bank[:], func=GELU, bias=bias[:, i : i + 1])
-                if by_slice:
+                if i == 0:
                     nc.vector.tensor_tensor(
                         out=result[:, cols], in0=resid[i][:].indirect(entries(s)), in1=act[:, cols], op=ADD
                     )
-                if i == TILES - 1:
-                    nc.sync.dma_start(out=out[i * P : (i + 1) * P, cols], in_=result[:, cols])
-            if i < EARLY:
-                nc.vector.tensor_tensor(out=result[:], in0=result[:], in1=act[:], op=ADD)
-            elif not by_slice:
+            if i > 0:
                 nc.vector.tensor_tensor(out=result[:], in0=resid[i][:].indirect(offsets[:]), in1=act[:], op=ADD)
-            if i == 1:
-                quantize_up(1, up_raw1, nc.scalar.copy)
-            if i < TILES - 1:
-                nc.sync.dma_start(out=out[i * P : (i + 1) * P, :], in_=result[:])
+            nc.sync.dma_start(out=out[rows, :], in_=result[:])

@@ -60,10 +60,10 @@ def tile_list_tabres_gelu_kernel(
 
         scale_window = keep.tile([P, T], U8, name="scale_window", align_bytes=ALIGN)
         w4_plane = keep.tile([P, PASSES, M], U8, name="w4_plane", align_bytes=ALIGN)
-        moved = keep.tile([P, PASSES - 1, S], U8, name="moved", align_bytes=ALIGN)
+        v_planes = keep.tile([P, PASSES, S], U8, name="v_planes", align_bytes=ALIGN)
         nc.vector.memset(scale_window[:].bitcast(I32), 0)
         nc.vector.memset(w4_plane[:].bitcast(I32), 0)
-        nc.vector.memset(moved[:].bitcast(I32), 0)
+        nc.vector.memset(v_planes[:].bitcast(I32), 0)
 
         down_raw = []
         for a in range(PASSES):
@@ -74,14 +74,16 @@ def tile_list_tabres_gelu_kernel(
             down_raw.append(raw)
             if a == 0:
                 nc.sync.dma_start(offsets[:], offs)
-                for q in range(QUADS):
-                    nc.gpsimd.dma_start(
-                        out=scale_window[QUAD * q : QUAD * q + PLANE_ROWS * PASSES, :].bitcast(I32),
-                        in_=tab_scales[:, PLANE_ROWS * q : PLANE_ROWS * (q + 1), :].bitcast(I32),
+                for c in range(PASSES):
+                    nc.sync.dma_start(
+                        out=scale_window[QUAD + c : 3 * QUAD : PLANE_ROWS, :].bitcast(I32),
+                        in_=tab_scales[c].bitcast(I32),
                     )
+        up_raw = slot(TILES - 1, [P, PACK, M], F32, "up_raw")
+        nc.sync.dma_start(out=up_raw[:], in_=up.rearrange("(p j) n -> p j n", j=PACK))
         b_rows = keep.tile([P, P], F32, name="b_rows")
         nc.gpsimd.memset(b_rows[:], 0.0)
-        nc.gpsimd.dma_start(out=b_rows[0:TILES, :], in_=b.rearrange("(c p) -> c p", p=P))
+        nc.gpsimd.dma_start(out=b_rows[GROUP : GROUP + TILES, :], in_=b.rearrange("(c p) -> c p", p=P))
         table = []
         for a in range(PASSES):
             words = slot(1 + PASSES + a, [P, T], U32, "table%d" % a)
@@ -96,8 +98,6 @@ def tile_list_tabres_gelu_kernel(
             )
         w4 = keep.tile([P, PASSES, 2 * M], U8, name="w4", align_bytes=ALIGN)
         nc.sync.dma_start(out=w4[:].bitcast(I32), in_=w4_words.rearrange("a p n -> p a n").bitcast(I32))
-        up_raw = slot(TILES - 1, [P, PACK, M], F32, "up_raw")
-        nc.sync.dma_start(out=up_raw[:], in_=up.rearrange("(p j) n -> p j n", j=PACK))
         resid = []
 
         def load_resid(i):
@@ -112,16 +112,16 @@ def tile_list_tabres_gelu_kernel(
         b_bank = psum.tile([P, BANK], F32, name="b_bank", tag="bank")
         nc.tensor.transpose(b_bank[:, 0:P], b_rows[:], ident[:])
         bias = keep.tile([P, TILES], F32, name="bias")
-        nc.scalar.copy(out=bias[:], in_=b_bank[:, 0:TILES])
+        nc.scalar.copy(out=bias[:], in_=b_bank[:, GROUP : GROUP + TILES])
 
-        v_plane = keep.tile([P, S], U8, name="v_plane", align_bytes=ALIGN)
-        nc.vector.tensor_copy(out=v_plane[:], in_=scale_window[:].indirect(offsets[:]))
-        for a in range(1, PASSES):
+        picked = keep.tile([P, S], U8, name="picked", align_bytes=ALIGN)
+        nc.vector.tensor_copy(out=picked[:], in_=scale_window[:].indirect(offsets[:]))
+        for a in range(PASSES):
             for q in range(QUADS):
-                first = QUAD * q + PLANE_ROWS * a
+                first = QUAD + a + PLANE_ROWS * PLANE_ROWS * q
                 nc.gpsimd.dma_start(
-                    out=moved[QUAD * q : QUAD * q + PLANE_ROWS, a - 1, :].bitcast(I32),
-                    in_=v_plane[first : first + PLANE_ROWS, :].bitcast(I32),
+                    out=v_planes[QUAD * q : QUAD * q + PLANE_ROWS, a, :].bitcast(I32),
+                    in_=picked[first : first + PLANE_ROWS * PLANE_ROWS : PLANE_ROWS, :].bitcast(I32),
                 )
 
         down_codes = []
@@ -138,6 +138,18 @@ def tile_list_tabres_gelu_kernel(
             down_codes.append(codes)
             down_planes.append(plane)
 
+        up_codes = keep.tile([P, M], U32, name="up_codes", align_bytes=ALIGN)
+        up_plane = keep.tile([P, M], U8, name="up_plane", align_bytes=ALIGN)
+
+        for half in range(2):
+            cols = slice(half * M // 2, (half + 1) * M // 2)
+            grouped = stage.tile([P, M // 2 * PACK], BF16, name="up_bf%d" % half, tag="grouped", align_bytes=ALIGN)
+            nc.scalar.copy(
+                out=grouped[:].rearrange("p (c i j) -> p c j i", i=LINE, j=PACK),
+                in_=up_raw[:, :, cols].rearrange("p j (c i) -> p c j i", i=LINE),
+            )
+            nc.vector.quantize_mx(out=up_codes[:, cols].bitcast(FP8X4), scales=up_plane[:, cols], in_=grouped[:])
+
         v_codes = []
         for a in range(PASSES):
             v_codes.append(keep.tile([P, S], U32, name="v_codes%d" % a, align_bytes=ALIGN))
@@ -148,7 +160,7 @@ def tile_list_tabres_gelu_kernel(
                 lhsT=down_codes[a][:, t * P : (t + 1) * P].bitcast(FP8X4),
                 lhsT_scale=down_planes[a][:, t * P : (t + 1) * P],
                 rhs=v_codes[a][:, cols].bitcast(FP8X4),
-                rhs_scale=v_plane[PLANE_ROWS * a : P, cols],
+                rhs_scale=v_planes[:, a, cols],
                 start=(a == 0),
                 stop=(a == PASSES - 1),
             )
@@ -165,19 +177,7 @@ def tile_list_tabres_gelu_kernel(
         for s in range(SLICES):
             nc.vector.tensor_copy(out=v_codes[last][:, token_cols(s)], in_=table[last][:].indirect(entries(s)))
 
-        up_codes = keep.tile([P, M], U32, name="up_codes", align_bytes=ALIGN)
-        up_plane = keep.tile([P, M], U8, name="up_plane", align_bytes=ALIGN)
-
-        def quantize_up(half, copy):
-            cols = slice(half * M // 2, (half + 1) * M // 2)
-            grouped = stage.tile([P, M // 2 * PACK], BF16, name="up_bf%d" % half, tag="grouped", align_bytes=ALIGN)
-            copy(
-                out=grouped[:].rearrange("p (c i j) -> p c j i", i=LINE, j=PACK),
-                in_=up_raw[:, :, cols].rearrange("p j (c i) -> p c j i", i=LINE),
-            )
-            nc.vector.quantize_mx(out=up_codes[:, cols].bitcast(FP8X4), scales=up_plane[:, cols], in_=grouped[:])
-
-        for i in range(1, TILES - 1):
+        for i in range(1, TILES):
             load_resid(i)
 
         h_codes = keep.tile([P, S], U32, name="h_codes", align_bytes=ALIGN)
@@ -205,10 +205,6 @@ def tile_list_tabres_gelu_kernel(
                         in_=shared[:].rearrange("p t n -> p n t"),
                     )
             nc.vector.quantize_mx(out=h_codes[:, cols].bitcast(FP8X4), scales=h_plane[:, cols], in_=grouped[:])
-            if s == 0:
-                quantize_up(0, nc.vector.tensor_copy)
-        quantize_up(1, nc.scalar.copy)
-        load_resid(TILES - 1)
 
         for i in range(TILES):
             rows = slice(i * P, (i + 1) * P)
@@ -223,7 +219,7 @@ def tile_list_tabres_gelu_kernel(
                         lhsT=w4[:, a, 2 * i * P : 2 * (i + 1) * P].bitcast(FP4X4),
                         lhsT_scale=w4_plane[:, a, rows],
                         rhs=v_codes[a][:, cols].bitcast(FP8X4),
-                        rhs_scale=v_plane[:, cols] if a == 0 else moved[:, a - 1, cols],
+                        rhs_scale=v_planes[:, a, cols],
                         start=(a == 0),
                         stop=False,
                     )

@@ -30,6 +30,8 @@ QUAD = P // QUADS
 PLANE_ROWS = 4
 GROUP = 16
 LINE = 4
+DEAL = 4
+HALVES = TILES // DEAL
 ALIGN = 64
 EARLY_SLICES = BANKS // PACK
 STAGE_BUFS = 6
@@ -59,15 +61,16 @@ def tile_list_tabres_gelu_kernel(
             return offsets[:, s * BANK // GROUP : (s + 1) * BANK // GROUP]
 
         scale_window = keep.tile([P, T], U8, name="scale_window", align_bytes=ALIGN)
-        w4_plane = keep.tile([P, PASSES, M], U8, name="w4_plane", align_bytes=ALIGN)
-        v_planes = keep.tile([P, PASSES, S], U8, name="v_planes", align_bytes=ALIGN)
+        w4_plane_raw = stage.tile([P, PASSES, M], U8, name="w4_plane_raw", tag="grouped", align_bytes=ALIGN, offset=0)
+        v_planes = [keep.tile([P, S], U8, name="v_plane%d" % a, align_bytes=ALIGN) for a in range(PASSES)]
         nc.vector.memset(scale_window[:].bitcast(I32), 0)
-        nc.vector.memset(w4_plane[:].bitcast(I32), 0)
-        nc.vector.memset(v_planes[:].bitcast(I32), 0)
+        nc.vector.memset(w4_plane_raw[:].bitcast(I32), 0)
+        for plane in v_planes:
+            nc.vector.memset(plane[:].bitcast(I32), 0)
 
         down_raw = []
         for a in range(PASSES):
-            raw = slot(1 + a, [P, PACK, R], F32, "down_raw%d" % a)
+            raw = slot(a, [P, PACK, R], F32, "down_raw%d" % a)
             nc.sync.dma_start(
                 out=raw[:], in_=down[a * K_PASS : (a + 1) * K_PASS, :].rearrange("(p j) r -> p j r", j=PACK)
             )
@@ -79,55 +82,55 @@ def tile_list_tabres_gelu_kernel(
                         out=scale_window[QUAD + c : 3 * QUAD : PLANE_ROWS, :].bitcast(I32),
                         in_=tab_scales[c].bitcast(I32),
                     )
-        up_raw = slot(TILES - 1, [P, PACK, M], F32, "up_raw")
+        w4_raw = slot(PASSES, [P, PASSES, 2 * M], U8, "w4_raw")
+        nc.sync.dma_start(out=w4_raw[:].bitcast(I32), in_=w4_words.rearrange("a p n -> p a n").bitcast(I32))
+        up_raw = slot(PASSES + 1, [P, PACK, M], F32, "up_raw")
         nc.sync.dma_start(out=up_raw[:], in_=up.rearrange("(p j) n -> p j n", j=PACK))
-        b_rows = keep.tile([P, P], F32, name="b_rows")
+        b_rows = keep.tile([P, DEAL * P], F32, name="b_rows")
         nc.gpsimd.memset(b_rows[:], 0.0)
-        nc.gpsimd.dma_start(out=b_rows[GROUP : GROUP + TILES, :], in_=b.rearrange("(c p) -> c p", p=P))
+        nc.gpsimd.dma_start(out=b_rows[GROUP : GROUP + HALVES, :], in_=b.rearrange("(g c) -> g c", g=HALVES))
         table = []
         for a in range(PASSES):
-            words = slot(1 + PASSES + a, [P, T], U32, "table%d" % a)
+            words = slot(PASSES + 2 + a, [P, T], U32, "table%d" % a)
             nc.sync.dma_start(
                 out=words[:].bitcast(I32), in_=tab_words[a].rearrange("p t i -> p (t i)").bitcast(I32)
             )
             table.append(words)
-        for q in range(QUADS):
+        for r in range(PLANE_ROWS):
             nc.gpsimd.dma_start(
-                out=w4_plane[QUAD * q : QUAD * q + PLANE_ROWS, :, :].bitcast(I32),
-                in_=w4_scales[:, PLANE_ROWS * q : PLANE_ROWS * (q + 1), :].rearrange("a r n -> r a n").bitcast(I32),
+                out=w4_plane_raw[r:P:QUAD, :, :].bitcast(I32),
+                in_=w4_scales[:, r::PLANE_ROWS, :].rearrange("a q n -> q a n").bitcast(I32),
             )
-        w4 = keep.tile([P, PASSES, 2 * M], U8, name="w4", align_bytes=ALIGN)
-        nc.sync.dma_start(out=w4[:].bitcast(I32), in_=w4_words.rearrange("a p n -> p a n").bitcast(I32))
         resid = []
 
         def load_resid(i):
             rows = slot(i, [P, T], F32, "resid%d" % i)
-            nc.sync.dma_start(out=rows[:], in_=rT[i * P : (i + 1) * P, :])
+            g, u = divmod(i, DEAL)
+            nc.sync.dma_start(out=rows[:], in_=rT[g * DEAL * P + u : (g + 1) * DEAL * P : DEAL, :])
             resid.append(rows)
-
-        load_resid(0)
 
         ident = keep.tile([P, P], F32, name="ident")
         make_identity(nc, ident[:])
-        b_bank = psum.tile([P, BANK], F32, name="b_bank", tag="bank")
-        nc.tensor.transpose(b_bank[:, 0:P], b_rows[:], ident[:])
-        bias = keep.tile([P, TILES], F32, name="bias")
-        nc.scalar.copy(out=bias[:], in_=b_bank[:, GROUP : GROUP + TILES])
+        b_bank = psum.tile([P, DEAL, P], F32, name="b_bank", tag="bank")
+        for u in range(DEAL):
+            nc.tensor.transpose(b_bank[:, u, :], b_rows[:, u::DEAL], ident[:])
+        bias = keep.tile([P, HALVES, DEAL], F32, name="bias")
+        nc.scalar.copy(out=bias[:], in_=b_bank[:, :, GROUP : GROUP + HALVES].rearrange("p u g -> p g u"))
 
         picked = keep.tile([P, S], U8, name="picked", align_bytes=ALIGN)
         nc.vector.tensor_copy(out=picked[:], in_=scale_window[:].indirect(offsets[:]))
         for a in range(PASSES):
-            for q in range(QUADS):
-                first = QUAD + a + PLANE_ROWS * PLANE_ROWS * q
+            for r in range(PLANE_ROWS):
+                first = QUAD + a + PLANE_ROWS * r
                 nc.gpsimd.dma_start(
-                    out=v_planes[QUAD * q : QUAD * q + PLANE_ROWS, a, :].bitcast(I32),
-                    in_=picked[first : first + PLANE_ROWS * PLANE_ROWS : PLANE_ROWS, :].bitcast(I32),
+                    out=v_planes[a][r:P:QUAD, :].bitcast(I32),
+                    in_=picked[first : 3 * QUAD : PLANE_ROWS * PLANE_ROWS, :].bitcast(I32),
                 )
 
         down_codes = []
         down_planes = []
         for a in range(PASSES):
-            grouped = stage.tile([P, R * PACK], BF16, name="down_bf%d" % a, tag="grouped", align_bytes=ALIGN)
+            grouped = stage.tile([P, R * PACK], BF16, name="down_bf%d" % a, tag="grouped", align_bytes=ALIGN, offset=0)
             nc.scalar.copy(
                 out=grouped[:].rearrange("p (t m j) -> p m t j", t=PACK, j=PACK),
                 in_=down_raw[a][:].rearrange("p j (m t) -> p m t j", t=PACK),
@@ -138,15 +141,26 @@ def tile_list_tabres_gelu_kernel(
             down_codes.append(codes)
             down_planes.append(plane)
 
+        w4 = keep.tile([P, PASSES, 2 * M], U8, name="w4", align_bytes=ALIGN)
+        w4_plane = keep.tile([P, PASSES, M], U8, name="w4_plane", align_bytes=ALIGN)
+        nc.vector.tensor_copy(
+            out=w4_plane[:].rearrange("p a (g u m) -> p (a g) u m", g=HALVES, u=DEAL),
+            in_=w4_plane_raw[:].rearrange("p a (g m u) -> p (a g) u m", g=HALVES, u=DEAL),
+        )
+        nc.vector.tensor_copy(
+            out=w4[:].bitcast(U16).rearrange("p a (g u m) -> p (a g) u m", g=HALVES, u=DEAL),
+            in_=w4_raw[:].bitcast(U16).rearrange("p a (g m u) -> p (a g) u m", g=HALVES, u=DEAL),
+        )
+
         up_codes = keep.tile([P, M], U32, name="up_codes", align_bytes=ALIGN)
         up_plane = keep.tile([P, M], U8, name="up_plane", align_bytes=ALIGN)
 
         for half in range(2):
             cols = slice(half * M // 2, (half + 1) * M // 2)
-            grouped = stage.tile([P, M // 2 * PACK], BF16, name="up_bf%d" % half, tag="grouped", align_bytes=ALIGN)
+            grouped = stage.tile([P, M // 2 * PACK], BF16, name="up_bf%d" % half, tag="grouped", align_bytes=ALIGN, offset=0)
             nc.scalar.copy(
-                out=grouped[:].rearrange("p (c i j) -> p c j i", i=LINE, j=PACK),
-                in_=up_raw[:, :, cols].rearrange("p j (c i) -> p c j i", i=LINE),
+                out=grouped[:].rearrange("p (u m j) -> p m u j", u=DEAL, j=PACK),
+                in_=up_raw[:, :, cols].rearrange("p j (m u) -> p m u j", u=DEAL),
             )
             nc.vector.quantize_mx(out=up_codes[:, cols].bitcast(FP8X4), scales=up_plane[:, cols], in_=grouped[:])
 
@@ -160,7 +174,7 @@ def tile_list_tabres_gelu_kernel(
                 lhsT=down_codes[a][:, t * P : (t + 1) * P].bitcast(FP8X4),
                 lhsT_scale=down_planes[a][:, t * P : (t + 1) * P],
                 rhs=v_codes[a][:, cols].bitcast(FP8X4),
-                rhs_scale=v_planes[:, a, cols],
+                rhs_scale=v_planes[a][:, cols],
                 start=(a == 0),
                 stop=(a == PASSES - 1),
             )
@@ -177,16 +191,16 @@ def tile_list_tabres_gelu_kernel(
         for s in range(SLICES):
             nc.vector.tensor_copy(out=v_codes[last][:, token_cols(s)], in_=table[last][:].indirect(entries(s)))
 
-        for i in range(1, TILES):
+        for i in range(TILES):
             load_resid(i)
 
         h_codes = keep.tile([P, S], U32, name="h_codes", align_bytes=ALIGN)
         h_plane = keep.tile([P, S], U8, name="h_plane", align_bytes=ALIGN)
         for s in range(SLICES):
             cols = token_cols(s)
-            grouped = stage.tile([P, BANK * PACK], BF16, name="h_bf%d" % s, tag="grouped", align_bytes=ALIGN)
+            grouped = stage.tile([P, BANK * PACK], BF16, name="h_bf%d" % s, tag="grouped", align_bytes=ALIGN, offset=0)
             if s < EARLY_SLICES:
-                apart = stage.tile([P, PACK, BANK], BF16, name="h_apart%d" % s, tag="grouped", align_bytes=ALIGN)
+                apart = stage.tile([P, PACK, BANK], BF16, name="h_apart%d" % s, tag="grouped", align_bytes=ALIGN, offset=0)
                 for t in range(PACK):
                     h_pass(early[s][t][:], t, last, cols)
                     nc.scalar.copy(out=apart[:, t, :], in_=early[s][t][:])
@@ -207,9 +221,16 @@ def tile_list_tabres_gelu_kernel(
             nc.vector.quantize_mx(out=h_codes[:, cols].bitcast(FP8X4), scales=h_plane[:, cols], in_=grouped[:])
 
         for i in range(TILES):
+            g, u = divmod(i, DEAL)
             rows = slice(i * P, (i + 1) * P)
             act = acts.tile([P, S], F32, name="act")
-            result = slot(i - 1 if i > 0 else TILES, [P, S], F32, "result%d" % i)
+            if i == 0:
+                first = i
+                results = stage.tile([P, DEAL, S], F32, name="results0", bufs=1, align_bytes=ALIGN, offset=0)
+            elif i >= DEAL and i % 2 == 0:
+                first = i
+                results = slot(i // 2 - 2, [P, 2, S], F32, "results%d" % i)
+            result = results[:, i - first, :]
             for s in range(SLICES):
                 cols = token_cols(s)
                 bank = psum.tile([P, BANK], F32, name="y_bank", tag="bank")
@@ -219,7 +240,7 @@ def tile_list_tabres_gelu_kernel(
                         lhsT=w4[:, a, 2 * i * P : 2 * (i + 1) * P].bitcast(FP4X4),
                         lhsT_scale=w4_plane[:, a, rows],
                         rhs=v_codes[a][:, cols].bitcast(FP8X4),
-                        rhs_scale=v_planes[:, a, cols],
+                        rhs_scale=v_planes[a][:, cols],
                         start=(a == 0),
                         stop=False,
                     )
@@ -232,11 +253,15 @@ def tile_list_tabres_gelu_kernel(
                     start=False,
                     stop=True,
                 )
-                nc.scalar.activation(out=act[:, cols], in_=bank[:], func=GELU, bias=bias[:, i : i + 1])
+                nc.scalar.activation(out=act[:, cols], in_=bank[:], func=GELU, bias=bias[:, g, u : u + 1])
                 if i == 0:
                     nc.vector.tensor_tensor(
                         out=result[:, cols], in0=resid[i][:].indirect(entries(s)), in1=act[:, cols], op=ADD
                     )
             if i > 0:
-                nc.vector.tensor_tensor(out=result[:], in0=resid[i][:].indirect(offsets[:]), in1=act[:], op=ADD)
-            nc.sync.dma_start(out=out[rows, :], in_=result[:])
+                nc.vector.tensor_tensor(out=result, in0=resid[i][:].indirect(offsets[:]), in1=act[:], op=ADD)
+            if i >= DEAL - 1 and i % 2 == 1:
+                dealt = out[g * DEAL * P : (g + 1) * DEAL * P, :].rearrange("(p u) s -> p (u s)", u=DEAL)
+                nc.sync.dma_start(
+                    out=dealt[:, (first % DEAL) * S : (u + 1) * S], in_=results[:].rearrange("p u s -> p (u s)")
+                )

@@ -82,20 +82,20 @@ def tile_list_tabres_gelu_kernel(
                         out=scale_window[QUAD + c : 3 * QUAD : PLANE_ROWS, :].bitcast(I32),
                         in_=tab_scales[c].bitcast(I32),
                     )
-        w4_raw = slot(PASSES, [P, PASSES, 2 * M], U8, "w4_raw")
-        nc.sync.dma_start(out=w4_raw[:].bitcast(I32), in_=w4_words.rearrange("a p n -> p a n").bitcast(I32))
-        up_raw = slot(PASSES + 1, [P, PACK, M], F32, "up_raw")
+        up_raw = slot(PASSES, [P, PACK, M], F32, "up_raw")
         nc.sync.dma_start(out=up_raw[:], in_=up.rearrange("(p j) n -> p j n", j=PACK))
         b_rows = keep.tile([P, DEAL * P], F32, name="b_rows")
         nc.gpsimd.memset(b_rows[:], 0.0)
         nc.gpsimd.dma_start(out=b_rows[GROUP : GROUP + HALVES, :], in_=b.rearrange("(g c) -> g c", g=HALVES))
         table = []
         for a in range(PASSES):
-            words = slot(PASSES + 2 + a, [P, T], U32, "table%d" % a)
+            words = slot(PASSES + 1 + a, [P, T], U32, "table%d" % a)
             nc.sync.dma_start(
                 out=words[:].bitcast(I32), in_=tab_words[a].rearrange("p t i -> p (t i)").bitcast(I32)
             )
             table.append(words)
+        w4_raw = slot(TILES - 1, [P, PASSES, 2 * M], U8, "w4_raw")
+        nc.sync.dma_start(out=w4_raw[:].bitcast(I32), in_=w4_words.rearrange("a p n -> p a n").bitcast(I32))
         for r in range(PLANE_ROWS):
             nc.gpsimd.dma_start(
                 out=w4_plane_raw[r:P:QUAD, :, :].bitcast(I32),
@@ -141,17 +141,6 @@ def tile_list_tabres_gelu_kernel(
             down_codes.append(codes)
             down_planes.append(plane)
 
-        w4 = keep.tile([P, PASSES, 2 * M], U8, name="w4", align_bytes=ALIGN)
-        w4_plane = keep.tile([P, PASSES, M], U8, name="w4_plane", align_bytes=ALIGN)
-        nc.vector.tensor_copy(
-            out=w4_plane[:].rearrange("p a (g u m) -> p (a g) u m", g=HALVES, u=DEAL),
-            in_=w4_plane_raw[:].rearrange("p a (g m u) -> p (a g) u m", g=HALVES, u=DEAL),
-        )
-        nc.vector.tensor_copy(
-            out=w4[:].bitcast(U16).rearrange("p a (g u m) -> p (a g) u m", g=HALVES, u=DEAL),
-            in_=w4_raw[:].bitcast(U16).rearrange("p a (g m u) -> p (a g) u m", g=HALVES, u=DEAL),
-        )
-
         up_codes = keep.tile([P, M], U32, name="up_codes", align_bytes=ALIGN)
         up_plane = keep.tile([P, M], U8, name="up_plane", align_bytes=ALIGN)
 
@@ -191,6 +180,17 @@ def tile_list_tabres_gelu_kernel(
         for s in range(SLICES):
             nc.vector.tensor_copy(out=v_codes[last][:, token_cols(s)], in_=table[last][:].indirect(entries(s)))
 
+        w4 = keep.tile([P, PASSES, 2 * M], U8, name="w4", align_bytes=ALIGN)
+        w4_plane = keep.tile([P, PASSES, M], U8, name="w4_plane", align_bytes=ALIGN)
+        nc.vector.tensor_copy(
+            out=w4_plane[:].rearrange("p a (g u m) -> p (a g) u m", g=HALVES, u=DEAL),
+            in_=w4_plane_raw[:].rearrange("p a (g m u) -> p (a g) u m", g=HALVES, u=DEAL),
+        )
+        nc.vector.tensor_copy(
+            out=w4[:].bitcast(U16).rearrange("p a (g u m) -> p (a g) u m", g=HALVES, u=DEAL),
+            in_=w4_raw[:].bitcast(U16).rearrange("p a (g m u) -> p (a g) u m", g=HALVES, u=DEAL),
+        )
+
         for i in range(TILES):
             load_resid(i)
 
@@ -227,9 +227,12 @@ def tile_list_tabres_gelu_kernel(
             if i == 0:
                 first = i
                 results = stage.tile([P, DEAL, S], F32, name="results0", bufs=1, align_bytes=ALIGN, offset=0)
-            elif i >= DEAL and i % 2 == 0:
+            elif i == DEAL:
                 first = i
-                results = slot(i // 2 - 2, [P, 2, S], F32, "results%d" % i)
+                results = slot(0, [P, 2, S], F32, "results%d" % i)
+            elif i > DEAL + 1:
+                first = i
+                results = slot(i - DEAL - 1, [P, 1, S], F32, "results%d" % i)
             result = results[:, i - first, :]
             for s in range(SLICES):
                 cols = token_cols(s)
@@ -260,7 +263,7 @@ def tile_list_tabres_gelu_kernel(
                     )
             if i > 0:
                 nc.vector.tensor_tensor(out=result, in0=resid[i][:].indirect(offsets[:]), in1=act[:], op=ADD)
-            if i >= DEAL - 1 and i % 2 == 1:
+            if i >= DEAL - 1 and i != DEAL:
                 dealt = out[g * DEAL * P : (g + 1) * DEAL * P, :].rearrange("(p u) s -> p (u s)", u=DEAL)
                 nc.sync.dma_start(
                     out=dealt[:, (first % DEAL) * S : (u + 1) * S], in_=results[:].rearrange("p u s -> p (u s)")

@@ -32,6 +32,7 @@ GROUP = 16
 LINE = 4
 DEAL = 4
 HALVES = TILES // DEAL
+BURST = 512
 ALIGN = 64
 EARLY_SLICES = BANKS // PACK
 STAGE_BUFS = 6
@@ -50,7 +51,7 @@ def tile_list_tabres_gelu_kernel(
         psum = ctx.enter_context(tc.psum_pool(name="psum", bufs=BANKS))
 
         def slot(n, shape, dtype, name):
-            return big.tile(shape, dtype, name=name, tag="slot%d" % n, align_bytes=ALIGN)
+            return big.tile(shape, dtype, name=name, tag="slot%d" % n, align_bytes=BURST)
 
         def token_cols(s):
             return slice(s * BANK, (s + 1) * BANK)
@@ -60,9 +61,9 @@ def tile_list_tabres_gelu_kernel(
         def entries(s):
             return offsets[:, s * BANK // GROUP : (s + 1) * BANK // GROUP]
 
-        scale_window = keep.tile([P, T], U8, name="scale_window", align_bytes=ALIGN)
+        scale_window = keep.tile([P, T], U8, name="scale_window", align_bytes=BURST)
         w4_plane_raw = stage.tile([P, PASSES, M], U8, name="w4_plane_raw", tag="grouped", align_bytes=ALIGN, offset=0)
-        v_planes = [keep.tile([P, S], U8, name="v_plane%d" % a, align_bytes=ALIGN) for a in range(PASSES)]
+        v_planes = [keep.tile([P, S], U8, name="v_plane%d" % a, align_bytes=BURST) for a in range(PASSES)]
         nc.vector.memset(scale_window[:].bitcast(I32), 0)
         nc.vector.memset(w4_plane_raw[:].bitcast(I32), 0)
         for plane in v_planes:
@@ -117,7 +118,7 @@ def tile_list_tabres_gelu_kernel(
         bias = keep.tile([P, HALVES, DEAL], F32, name="bias")
         nc.scalar.copy(out=bias[:], in_=b_bank[:, :, GROUP : GROUP + HALVES].rearrange("p u g -> p g u"))
 
-        picked = keep.tile([P, S], U8, name="picked", align_bytes=ALIGN)
+        picked = keep.tile([P, S], U8, name="picked", align_bytes=BURST)
         nc.vector.tensor_copy(out=picked[:], in_=scale_window[:].indirect(offsets[:]))
         for a in range(PASSES):
             for r in range(PLANE_ROWS):
@@ -226,7 +227,7 @@ def tile_list_tabres_gelu_kernel(
             act = acts.tile([P, S], F32, name="act")
             if i == 0:
                 first = i
-                results = stage.tile([P, DEAL, S], F32, name="results0", bufs=1, align_bytes=ALIGN, offset=0)
+                results = stage.tile([P, DEAL, S], F32, name="results0", bufs=1, align_bytes=BURST, offset=0)
             elif i == DEAL:
                 first = i
                 results = slot(0, [P, 2, S], F32, "results%d" % i)

@@ -25,17 +25,18 @@ BANK = 512
 BANKS = 8
 SLICES = S // BANK
 TILES = M // P
-QUADS = 4
-QUAD = P // QUADS
+QUAD = 32
 PLANE_ROWS = 4
 GROUP = 16
 LINE = 4
 DEAL = 4
 HALVES = TILES // DEAL
+HALF = M // HALVES
 BURST = 512
 ALIGN = 64
+REGION = 4 * T
 EARLY_SLICES = BANKS // PACK
-STAGE_BUFS = 6
+STAGE_BUFS = 7
 ACT_BUFS = 3
 
 
@@ -50,8 +51,8 @@ def tile_list_tabres_gelu_kernel(
         acts = ctx.enter_context(tc.tile_pool(name="acts", bufs=ACT_BUFS))
         psum = ctx.enter_context(tc.psum_pool(name="psum", bufs=BANKS))
 
-        def slot(n, shape, dtype, name):
-            return big.tile(shape, dtype, name=name, tag="slot%d" % n, align_bytes=BURST)
+        def tenant(region, shape, dtype, name, at=0):
+            return big.tile(shape, dtype, name=name, align_bytes=BURST, offset=region * REGION + at)
 
         def token_cols(s):
             return slice(s * BANK, (s + 1) * BANK)
@@ -61,54 +62,49 @@ def tile_list_tabres_gelu_kernel(
         def entries(s):
             return offsets[:, s * BANK // GROUP : (s + 1) * BANK // GROUP]
 
-        scale_window = keep.tile([P, T], U8, name="scale_window", align_bytes=BURST)
-        w4_plane_raw = stage.tile([P, PASSES, M], U8, name="w4_plane_raw", tag="grouped", align_bytes=ALIGN, offset=0)
+        window = tenant(3, [P, T], U8, "window", at=-T // 2)
+        w4_plane_raw = keep.tile([P, PASSES, M], U8, name="w4_plane_raw", align_bytes=BURST)
         v_planes = [keep.tile([P, S], U8, name="v_plane%d" % a, align_bytes=BURST) for a in range(PASSES)]
-        nc.vector.memset(scale_window[:].bitcast(I32), 0)
+        nc.vector.memset(window[:].bitcast(I32), 0)
         nc.vector.memset(w4_plane_raw[:].bitcast(I32), 0)
         for plane in v_planes:
             nc.vector.memset(plane[:].bitcast(I32), 0)
 
         down_raw = []
-        for a in range(PASSES):
-            raw = slot(a, [P, PACK, R], F32, "down_raw%d" % a)
+
+        def load_down(a, region, at):
+            raw = tenant(region, [P, PACK, R], F32, "down_raw%d" % a, at=at)
             nc.sync.dma_start(
                 out=raw[:], in_=down[a * K_PASS : (a + 1) * K_PASS, :].rearrange("(p j) r -> p j r", j=PACK)
             )
             down_raw.append(raw)
-            if a == 0:
-                nc.sync.dma_start(offsets[:], offs)
-                for c in range(PASSES):
-                    nc.sync.dma_start(
-                        out=scale_window[QUAD + c : 3 * QUAD : PLANE_ROWS, :].bitcast(I32),
-                        in_=tab_scales[c].bitcast(I32),
-                    )
-        up_raw = slot(PASSES, [P, PACK, M], F32, "up_raw")
-        nc.sync.dma_start(out=up_raw[:], in_=up.rearrange("(p j) n -> p j n", j=PACK))
-        b_rows = keep.tile([P, DEAL * P], F32, name="b_rows")
-        nc.gpsimd.memset(b_rows[:], 0.0)
-        nc.gpsimd.dma_start(out=b_rows[GROUP : GROUP + HALVES, :], in_=b.rearrange("(g c) -> g c", g=HALVES))
+
         table = []
-        for a in range(PASSES):
-            words = slot(PASSES + 1 + a, [P, T], U32, "table%d" % a)
+
+        def load_table(a):
+            words = tenant(a, [P, T], U32, "table%d" % a)
             nc.sync.dma_start(
                 out=words[:].bitcast(I32), in_=tab_words[a].rearrange("p t i -> p (t i)").bitcast(I32)
             )
             table.append(words)
-        w4_raw = slot(TILES - 1, [P, PASSES, 2 * M], U8, "w4_raw")
-        nc.sync.dma_start(out=w4_raw[:].bitcast(I32), in_=w4_words.rearrange("a p n -> p a n").bitcast(I32))
+
+        load_down(0, 4, 0)
+        nc.sync.dma_start(offsets[:], offs)
+        for c in range(PASSES):
+            nc.sync.dma_start(
+                out=window[QUAD + c : 3 * QUAD : PLANE_ROWS, :].bitcast(I32), in_=tab_scales[c].bitcast(I32)
+            )
+        load_table(0)
+        load_table(1)
+        load_down(1, 4, REGION // 2)
+        b_rows = keep.tile([P, DEAL * P], F32, name="b_rows")
+        nc.gpsimd.memset(b_rows[:], 0.0)
+        nc.gpsimd.dma_start(out=b_rows[GROUP : GROUP + HALVES, :], in_=b.rearrange("(g c) -> g c", g=HALVES))
         for r in range(PLANE_ROWS):
             nc.gpsimd.dma_start(
                 out=w4_plane_raw[r:P:QUAD, :, :].bitcast(I32),
                 in_=w4_scales[:, r::PLANE_ROWS, :].rearrange("a q n -> q a n").bitcast(I32),
             )
-        resid = []
-
-        def load_resid(i):
-            rows = slot(i, [P, T], F32, "resid%d" % i)
-            g, u = divmod(i, DEAL)
-            nc.sync.dma_start(out=rows[:], in_=rT[g * DEAL * P + u : (g + 1) * DEAL * P : DEAL, :])
-            resid.append(rows)
 
         ident = keep.tile([P, P], F32, name="ident")
         make_identity(nc, ident[:])
@@ -119,19 +115,45 @@ def tile_list_tabres_gelu_kernel(
         nc.scalar.copy(out=bias[:], in_=b_bank[:, :, GROUP : GROUP + HALVES].rearrange("p u g -> p g u"))
 
         picked = keep.tile([P, S], U8, name="picked", align_bytes=BURST)
-        nc.vector.tensor_copy(out=picked[:], in_=scale_window[:].indirect(offsets[:]))
-        for a in range(PASSES):
+        nc.vector.tensor_copy(out=picked[:], in_=window[:].indirect(offsets[:]))
+
+        def move_plane(a, queue):
             for r in range(PLANE_ROWS):
                 first = QUAD + a + PLANE_ROWS * r
-                nc.gpsimd.dma_start(
+                queue.dma_start(
                     out=v_planes[a][r:P:QUAD, :].bitcast(I32),
                     in_=picked[first : 3 * QUAD : PLANE_ROWS * PLANE_ROWS, :].bitcast(I32),
                 )
 
+        move_plane(0, nc.sync)
+        load_down(2, 3, 0)
+        move_plane(1, nc.sync)
+        load_table(2)
+        move_plane(2, nc.gpsimd)
+
+        v_codes = []
+        for a in range(PASSES):
+            codes = keep.tile([P, S], U32, name="v_codes%d" % a, align_bytes=ALIGN)
+            if a < PASSES - 1:
+                nc.vector.tensor_copy(out=codes[:], in_=table[a][:].indirect(offsets[:]))
+            else:
+                for s in range(SLICES):
+                    nc.vector.tensor_copy(out=codes[:, token_cols(s)], in_=table[a][:].indirect(entries(s)))
+            v_codes.append(codes)
+
+        up_raw = tenant(0, [P, PACK, M], F32, "up_raw")
+        nc.sync.dma_start(out=up_raw[:], in_=up.rearrange("(p j) n -> p j n", j=PACK))
+        w4_raw = tenant(1, [P, PASSES, 2 * M], U8, "w4_raw")
+        nc.sync.dma_start(out=w4_raw[:].bitcast(I32), in_=w4_words.rearrange("a p n -> p a n").bitcast(I32))
+
+        def staging(name, shape):
+            return stage.tile(shape, BF16, name=name, tag="staging", align_bytes=ALIGN)
+
         down_codes = []
         down_planes = []
-        for a in range(PASSES):
-            grouped = stage.tile([P, R * PACK], BF16, name="down_bf%d" % a, tag="grouped", align_bytes=ALIGN, offset=0)
+
+        def quantise_down(a):
+            grouped = staging("down_bf%d" % a, [P, R * PACK])
             nc.scalar.copy(
                 out=grouped[:].rearrange("p (t m j) -> p m t j", t=PACK, j=PACK),
                 in_=down_raw[a][:].rearrange("p j (m t) -> p m t j", t=PACK),
@@ -142,107 +164,125 @@ def tile_list_tabres_gelu_kernel(
             down_codes.append(codes)
             down_planes.append(plane)
 
-        up_codes = keep.tile([P, M], U32, name="up_codes", align_bytes=ALIGN)
-        up_plane = keep.tile([P, M], U8, name="up_plane", align_bytes=ALIGN)
-
-        for half in range(2):
-            cols = slice(half * M // 2, (half + 1) * M // 2)
-            grouped = stage.tile([P, M // 2 * PACK], BF16, name="up_bf%d" % half, tag="grouped", align_bytes=ALIGN, offset=0)
-            nc.scalar.copy(
-                out=grouped[:].rearrange("p (u m j) -> p m u j", u=DEAL, j=PACK),
-                in_=up_raw[:, :, cols].rearrange("p j (m u) -> p m u j", u=DEAL),
-            )
-            nc.vector.quantize_mx(out=up_codes[:, cols].bitcast(FP8X4), scales=up_plane[:, cols], in_=grouped[:])
-
-        v_codes = []
-        for a in range(PASSES):
-            v_codes.append(keep.tile([P, S], U32, name="v_codes%d" % a, align_bytes=ALIGN))
-
-        def h_pass(sums, t, a, cols):
+        def h_pass(sums, t, a, cols, start, stop):
             nc.tensor.matmul_mx(
                 out=sums,
                 lhsT=down_codes[a][:, t * P : (t + 1) * P].bitcast(FP8X4),
                 lhsT_scale=down_planes[a][:, t * P : (t + 1) * P],
                 rhs=v_codes[a][:, cols].bitcast(FP8X4),
                 rhs_scale=v_planes[a][:, cols],
-                start=(a == 0),
-                stop=(a == PASSES - 1),
+                start=start,
+                stop=stop,
             )
 
         last = PASSES - 1
-        early = []
-        for s in range(EARLY_SLICES):
-            early.append([psum.tile([P, BANK], F32, name="h_early%d_%d" % (s, t), tag="bank") for t in range(PACK)])
-        for a in range(last):
-            nc.vector.tensor_copy(out=v_codes[a][:], in_=table[a][:].indirect(offsets[:]))
-            for s in range(EARLY_SLICES):
-                for t in range(PACK):
-                    h_pass(early[s][t][:], t, a, token_cols(s))
-        for s in range(SLICES):
-            nc.vector.tensor_copy(out=v_codes[last][:, token_cols(s)], in_=table[last][:].indirect(entries(s)))
+        chunks = [psum.tile([P, PACK, P], F32, name="h_chunk%d" % c, tag="bank") for c in range(BANKS)]
 
-        w4 = keep.tile([P, PASSES, 2 * M], U8, name="w4", align_bytes=ALIGN)
-        w4_plane = keep.tile([P, PASSES, M], U8, name="w4_plane", align_bytes=ALIGN)
-        nc.vector.tensor_copy(
-            out=w4_plane[:].rearrange("p a (g u m) -> p (a g) u m", g=HALVES, u=DEAL),
-            in_=w4_plane_raw[:].rearrange("p a (g m u) -> p (a g) u m", g=HALVES, u=DEAL),
-        )
-        nc.vector.tensor_copy(
-            out=w4[:].bitcast(U16).rearrange("p a (g u m) -> p (a g) u m", g=HALVES, u=DEAL),
-            in_=w4_raw[:].bitcast(U16).rearrange("p a (g m u) -> p (a g) u m", g=HALVES, u=DEAL),
-        )
+        def chunk_pass(c, a):
+            for t in range(PACK):
+                h_pass(
+                    chunks[c][:, t, :], t, a, slice(c * P, (c + 1) * P), a == 0 and t == 0, a == last and t == PACK - 1
+                )
 
-        for i in range(TILES):
-            load_resid(i)
+        for a in range(PASSES):
+            quantise_down(a)
+            if a < last:
+                for c in range(BANKS):
+                    chunk_pass(c, a)
+
+        w4 = []
+        w4_plane = []
+
+        def deal_w4(g):
+            words = keep.tile([P, PASSES, 2 * HALF], U8, name="w4_%d" % g, align_bytes=ALIGN)
+            plane = keep.tile([P, PASSES, HALF], U8, name="w4_plane%d" % g, align_bytes=ALIGN)
+            nc.vector.tensor_copy(
+                out=plane[:].rearrange("p a (u m) -> p u a m", u=DEAL),
+                in_=w4_plane_raw[:, :, g * HALF : (g + 1) * HALF].rearrange("p a (m u) -> p u a m", u=DEAL),
+            )
+            nc.vector.tensor_copy(
+                out=words[:].bitcast(U16).rearrange("p a (u m) -> p u a m", u=DEAL),
+                in_=w4_raw[:].bitcast(U16)[:, :, g * HALF : (g + 1) * HALF].rearrange("p a (m u) -> p u a m", u=DEAL),
+            )
+            w4.append(words)
+            w4_plane.append(plane)
+
+        up_codes = []
+        up_planes = []
+
+        def quantise_up(g):
+            grouped = staging("up_bf%d" % g, [P, HALF * PACK])
+            nc.scalar.copy(
+                out=grouped[:].rearrange("p (u m j) -> p m u j", u=DEAL, j=PACK),
+                in_=up_raw[:, :, g * HALF : (g + 1) * HALF].rearrange("p j (m u) -> p m u j", u=DEAL),
+            )
+            codes = keep.tile([P, HALF], U32, name="up_codes%d" % g, align_bytes=ALIGN)
+            plane = keep.tile([P, HALF], U8, name="up_plane%d" % g, align_bytes=ALIGN)
+            nc.vector.quantize_mx(out=codes[:].bitcast(FP8X4), scales=plane[:], in_=grouped[:])
+            up_codes.append(codes)
+            up_planes.append(plane)
 
         h_codes = keep.tile([P, S], U32, name="h_codes", align_bytes=ALIGN)
         h_plane = keep.tile([P, S], U8, name="h_plane", align_bytes=ALIGN)
         for s in range(SLICES):
             cols = token_cols(s)
-            grouped = stage.tile([P, BANK * PACK], BF16, name="h_bf%d" % s, tag="grouped", align_bytes=ALIGN, offset=0)
+            grouped = staging("h_bf%d" % s, [P, BANK * PACK])
             if s < EARLY_SLICES:
-                apart = stage.tile([P, PACK, BANK], BF16, name="h_apart%d" % s, tag="grouped", align_bytes=ALIGN, offset=0)
+                for c in range(BANK // P):
+                    chunk_pass(s * BANK // P + c, last)
+                    nc.scalar.copy(
+                        out=grouped[:, c * P * PACK : (c + 1) * P * PACK].rearrange("p (n t) -> p n t", t=PACK),
+                        in_=chunks[s * BANK // P + c][:].rearrange("p t n -> p n t"),
+                    )
+            else:
+                apart = staging("h_apart", [P, PACK, BANK])
                 for t in range(PACK):
-                    h_pass(early[s][t][:], t, last, cols)
-                    nc.scalar.copy(out=apart[:, t, :], in_=early[s][t][:])
+                    bank = psum.tile([P, BANK], F32, name="h_late", tag="bank")
+                    for a in range(PASSES):
+                        h_pass(bank[:], t, a, cols, a == 0, a == last)
+                    nc.scalar.copy(out=apart[:, t, :], in_=bank[:])
                 nc.vector.tensor_copy(
                     out=grouped[:].rearrange("p (c i t) -> p c t i", i=LINE, t=PACK),
                     in_=apart[:].rearrange("p t (c i) -> p c t i", i=LINE),
                 )
-            else:
-                for c in range(BANK // P):
-                    shared = psum.tile([P, PACK, P], F32, name="h_shared", tag="bank")
-                    for t in range(PACK):
-                        for a in range(PASSES):
-                            h_pass(shared[:, t, :], t, a, slice(s * BANK + c * P, s * BANK + (c + 1) * P))
-                    nc.scalar.copy(
-                        out=grouped[:, c * P * PACK : (c + 1) * P * PACK].rearrange("p (n t) -> p n t", t=PACK),
-                        in_=shared[:].rearrange("p t n -> p n t"),
-                    )
             nc.vector.quantize_mx(out=h_codes[:, cols].bitcast(FP8X4), scales=h_plane[:, cols], in_=grouped[:])
+            if s == 0:
+                quantise_up(0)
+                deal_w4(0)
+
+        resid = []
+
+        def load_resid(i):
+            rows = tenant((4, 3, 2, 1, 0)[i % 5], [P, T], F32, "resid%d" % i)
+            g, u = divmod(i, DEAL)
+            nc.sync.dma_start(out=rows[:], in_=rT[g * DEAL * P + u : (g + 1) * DEAL * P : DEAL, :])
+            resid.append(rows)
+
+        for i in range(3):
+            load_resid(i)
+
+        results = [keep.tile([P, DEAL, S], F32, name="results%d" % g, align_bytes=BURST) for g in range(HALVES)]
+
+        def store(g, first, end):
+            dealt = out[g * HALF : (g + 1) * HALF, :].rearrange("(p u) s -> p (u s)", u=DEAL)
+            nc.sync.dma_start(
+                out=dealt[:, first * S : end * S],
+                in_=results[g][:].rearrange("p u s -> p (u s)")[:, first * S : end * S],
+            )
 
         for i in range(TILES):
             g, u = divmod(i, DEAL)
-            rows = slice(i * P, (i + 1) * P)
+            rows = slice(u * P, (u + 1) * P)
             act = acts.tile([P, S], F32, name="act")
-            if i == 0:
-                first = i
-                results = stage.tile([P, DEAL, S], F32, name="results0", bufs=1, align_bytes=BURST, offset=0)
-            elif i == DEAL:
-                first = i
-                results = slot(0, [P, 2, S], F32, "results%d" % i)
-            elif i > DEAL + 1:
-                first = i
-                results = slot(i - DEAL - 1, [P, 1, S], F32, "results%d" % i)
-            result = results[:, i - first, :]
+            result = results[g][:, u, :]
             for s in range(SLICES):
                 cols = token_cols(s)
                 bank = psum.tile([P, BANK], F32, name="y_bank", tag="bank")
                 for a in range(PASSES):
                     nc.tensor.matmul_mx(
                         out=bank[:],
-                        lhsT=w4[:, a, 2 * i * P : 2 * (i + 1) * P].bitcast(FP4X4),
-                        lhsT_scale=w4_plane[:, a, rows],
+                        lhsT=w4[g][:, a, 2 * u * P : 2 * (u + 1) * P].bitcast(FP4X4),
+                        lhsT_scale=w4_plane[g][:, a, rows],
                         rhs=v_codes[a][:, cols].bitcast(FP8X4),
                         rhs_scale=v_planes[a][:, cols],
                         start=(a == 0),
@@ -250,8 +290,8 @@ def tile_list_tabres_gelu_kernel(
                     )
                 nc.tensor.matmul_mx(
                     out=bank[:],
-                    lhsT=up_codes[:, rows].bitcast(FP8X4),
-                    lhsT_scale=up_plane[:, rows],
+                    lhsT=up_codes[g][:, rows].bitcast(FP8X4),
+                    lhsT_scale=up_planes[g][:, rows],
                     rhs=h_codes[:, cols].bitcast(FP8X4),
                     rhs_scale=h_plane[:, cols],
                     start=False,
@@ -264,8 +304,15 @@ def tile_list_tabres_gelu_kernel(
                     )
             if i > 0:
                 nc.vector.tensor_tensor(out=result, in0=resid[i][:].indirect(offsets[:]), in1=act[:], op=ADD)
-            if i >= DEAL - 1 and i != DEAL:
-                dealt = out[g * DEAL * P : (g + 1) * DEAL * P, :].rearrange("(p u) s -> p (u s)", u=DEAL)
-                nc.sync.dma_start(
-                    out=dealt[:, (first % DEAL) * S : (u + 1) * S], in_=results[:].rearrange("p u s -> p (u s)")
-                )
+            if i == 0:
+                deal_w4(1)
+                load_resid(3)
+                quantise_up(1)
+                load_resid(4)
+            if i + 5 < TILES:
+                load_resid(i + 5)
+            if i == DEAL - 1:
+                store(0, 0, DEAL)
+            if i == TILES - 2:
+                store(1, 0, DEAL - 1)
+        store(1, DEAL - 1, DEAL)

@@ -62,7 +62,7 @@ def tile_list_tabres_gelu_kernel(
         def entries(s):
             return offsets[:, s * BANK // GROUP : (s + 1) * BANK // GROUP]
 
-        window = tenant(3, [P, T], U8, "window", at=-T // 2)
+        window = tenant(2, [P, T], U8, "window", at=-T // 2)
         w4_plane_raw = keep.tile([P, PASSES, M], U8, name="w4_plane_raw", align_bytes=BURST)
         v_planes = [keep.tile([P, S], U8, name="v_plane%d" % a, align_bytes=BURST) for a in range(PASSES)]
         nc.vector.memset(window[:].bitcast(I32), 0)
@@ -88,18 +88,18 @@ def tile_list_tabres_gelu_kernel(
             )
             table.append(words)
 
-        load_down(0, 4, 0)
+        load_down(0, 3, 0)
         nc.sync.dma_start(offsets[:], offs)
         for c in range(PASSES):
             nc.sync.dma_start(
                 out=window[QUAD + c : 3 * QUAD : PLANE_ROWS, :].bitcast(I32), in_=tab_scales[c].bitcast(I32)
             )
+        load_down(1, 3, REGION // 2)
+        load_down(2, 4, 0)
         load_table(0)
-        load_table(1)
-        load_down(1, 4, REGION // 2)
         b_rows = keep.tile([P, DEAL * P], F32, name="b_rows")
         nc.gpsimd.memset(b_rows[:], 0.0)
-        nc.gpsimd.dma_start(out=b_rows[GROUP : GROUP + HALVES, :], in_=b.rearrange("(g c) -> g c", g=HALVES))
+        nc.scalar.dma_start(out=b_rows[GROUP : GROUP + HALVES, :], in_=b.rearrange("(g c) -> g c", g=HALVES))
         for r in range(PLANE_ROWS):
             nc.gpsimd.dma_start(
                 out=w4_plane_raw[r:P:QUAD, :, :].bitcast(I32),
@@ -117,19 +117,18 @@ def tile_list_tabres_gelu_kernel(
         picked = keep.tile([P, S], U8, name="picked", align_bytes=BURST)
         nc.vector.tensor_copy(out=picked[:], in_=window[:].indirect(offsets[:]))
 
-        def move_plane(a, queue):
+        def move_plane(a):
             for r in range(PLANE_ROWS):
                 first = QUAD + a + PLANE_ROWS * r
-                queue.dma_start(
+                nc.sync.dma_start(
                     out=v_planes[a][r:P:QUAD, :].bitcast(I32),
                     in_=picked[first : 3 * QUAD : PLANE_ROWS * PLANE_ROWS, :].bitcast(I32),
                 )
 
-        move_plane(0, nc.sync)
-        load_down(2, 3, 0)
-        move_plane(1, nc.sync)
-        load_table(2)
-        move_plane(2, nc.gpsimd)
+        for a in range(PASSES):
+            move_plane(a)
+            if a + 1 < PASSES:
+                load_table(a + 1)
 
         v_codes = []
         for a in range(PASSES):
@@ -140,11 +139,6 @@ def tile_list_tabres_gelu_kernel(
                 for s in range(SLICES):
                     nc.vector.tensor_copy(out=codes[:, token_cols(s)], in_=table[a][:].indirect(entries(s)))
             v_codes.append(codes)
-
-        up_raw = tenant(0, [P, PACK, M], F32, "up_raw")
-        nc.sync.dma_start(out=up_raw[:], in_=up.rearrange("(p j) n -> p j n", j=PACK))
-        w4_raw = tenant(1, [P, PASSES, 2 * M], U8, "w4_raw")
-        nc.sync.dma_start(out=w4_raw[:].bitcast(I32), in_=w4_words.rearrange("a p n -> p a n").bitcast(I32))
 
         def staging(name, shape):
             return stage.tile(shape, BF16, name=name, tag="staging", align_bytes=ALIGN)
@@ -189,6 +183,11 @@ def tile_list_tabres_gelu_kernel(
             if a < last:
                 for c in range(BANKS):
                     chunk_pass(c, a)
+
+        up_raw = tenant(3, [P, PACK, M], F32, "up_raw")
+        nc.sync.dma_start(out=up_raw[:], in_=up.rearrange("(p j) n -> p j n", j=PACK))
+        w4_raw = tenant(4, [P, PASSES, 2 * M], U8, "w4_raw")
+        nc.sync.dma_start(out=w4_raw[:].bitcast(I32), in_=w4_words.rearrange("a p n -> p a n").bitcast(I32))
 
         w4 = []
         w4_plane = []
@@ -253,12 +252,14 @@ def tile_list_tabres_gelu_kernel(
         resid = []
 
         def load_resid(i):
-            rows = tenant((4, 3, 2, 1, 0)[i % 5], [P, T], F32, "resid%d" % i)
+            rows = tenant((0, 1, 2, 4, 3)[i % 5], [P, T], F32, "resid%d" % i)
             g, u = divmod(i, DEAL)
             nc.sync.dma_start(out=rows[:], in_=rT[g * DEAL * P + u : (g + 1) * DEAL * P : DEAL, :])
             resid.append(rows)
 
-        for i in range(3):
+        deal_w4(1)
+        quantise_up(1)
+        for i in range(5):
             load_resid(i)
 
         results = [keep.tile([P, DEAL, S], F32, name="results%d" % g, align_bytes=BURST) for g in range(HALVES)]
@@ -304,11 +305,6 @@ def tile_list_tabres_gelu_kernel(
                     )
             if i > 0:
                 nc.vector.tensor_tensor(out=result, in0=resid[i][:].indirect(offsets[:]), in1=act[:], op=ADD)
-            if i == 0:
-                deal_w4(1)
-                load_resid(3)
-                quantise_up(1)
-                load_resid(4)
             if i + 5 < TILES:
                 load_resid(i + 5)
             if i == DEAL - 1:

@@ -35,8 +35,11 @@ HALF = M // HALVES
 BURST = 512
 ALIGN = 64
 REGION = 4 * T
+RESULTS = 4 * DEAL * S
+STAGE = 2 * PACK * BANK
+REGIONS = 5
+NICHE = PASSES * HALF
 EARLY_SLICES = BANKS // PACK
-STAGE_BUFS = 7
 ACT_BUFS = 3
 
 
@@ -47,12 +50,20 @@ def tile_list_tabres_gelu_kernel(
     with ExitStack() as ctx:
         keep = ctx.enter_context(tc.tile_pool(name="keep", bufs=1))
         big = ctx.enter_context(tc.tile_pool(name="big", bufs=1))
-        stage = ctx.enter_context(tc.tile_pool(name="stage", bufs=STAGE_BUFS))
         acts = ctx.enter_context(tc.tile_pool(name="acts", bufs=ACT_BUFS))
         psum = ctx.enter_context(tc.psum_pool(name="psum", bufs=BANKS))
 
-        def tenant(region, shape, dtype, name, at=0):
-            return big.tile(shape, dtype, name=name, align_bytes=BURST, offset=region * REGION + at)
+        def placed(offset, shape, dtype, name):
+            return big.tile(shape, dtype, name=name, align_bytes=BURST, offset=offset)
+
+        def region(n):
+            return n * REGION + min(n, 2) * NICHE
+
+        def results_at(g):
+            return region(REGIONS) + g * RESULTS
+
+        def staging(n, place, name, shape):
+            return placed(region(n) + place * STAGE, shape, BF16, name)
 
         def token_cols(s):
             return slice(s * BANK, (s + 1) * BANK)
@@ -62,7 +73,7 @@ def tile_list_tabres_gelu_kernel(
         def entries(s):
             return offsets[:, s * BANK // GROUP : (s + 1) * BANK // GROUP]
 
-        window = tenant(2, [P, T], U8, "window", at=-T // 2)
+        window = placed(region(2) - T // 2, [P, T], U8, "window")
         w4_plane_raw = keep.tile([P, PASSES, M], U8, name="w4_plane_raw", align_bytes=BURST)
         v_planes = [keep.tile([P, S], U8, name="v_plane%d" % a, align_bytes=BURST) for a in range(PASSES)]
         nc.vector.memset(window[:].bitcast(I32), 0)
@@ -70,32 +81,24 @@ def tile_list_tabres_gelu_kernel(
         for plane in v_planes:
             nc.vector.memset(plane[:].bitcast(I32), 0)
 
-        down_raw = []
-
-        def load_down(a, region, at):
-            raw = tenant(region, [P, PACK, R], F32, "down_raw%d" % a, at=at)
-            nc.sync.dma_start(
-                out=raw[:], in_=down[a * K_PASS : (a + 1) * K_PASS, :].rearrange("(p j) r -> p j r", j=PACK)
-            )
-            down_raw.append(raw)
-
-        table = []
-
-        def load_table(a):
-            words = tenant(a, [P, T], U32, "table%d" % a)
-            nc.sync.dma_start(
-                out=words[:].bitcast(I32), in_=tab_words[a].rearrange("p t i -> p (t i)").bitcast(I32)
-            )
-            table.append(words)
-
-        load_down(0, 3, 0)
+        w4_raw = placed(results_at(0) + PASSES * STAGE, [P, PASSES, 2 * M], U8, "w4_raw")
+        nc.sync.dma_start(out=w4_raw[:].bitcast(I32), in_=w4_words.rearrange("a p n -> p a n").bitcast(I32))
         nc.sync.dma_start(offsets[:], offs)
         for c in range(PASSES):
             nc.sync.dma_start(
                 out=window[QUAD + c : 3 * QUAD : PLANE_ROWS, :].bitcast(I32), in_=tab_scales[c].bitcast(I32)
             )
-        load_down(1, 3, REGION // 2)
-        load_down(2, 4, 0)
+        down_raw = placed(results_at(1), [P, PASSES, PACK * R], F32, "down_raw")
+        nc.sync.dma_start(out=down_raw[:], in_=down.rearrange("(a p j) r -> p a (j r)", p=P, j=PACK))
+        table = []
+
+        def load_table(a):
+            words = placed(region(a) + (NICHE if a < HALVES else 0), [P, T], U32, "table%d" % a)
+            nc.sync.dma_start(
+                out=words[:].bitcast(I32), in_=tab_words[a].rearrange("p t i -> p (t i)").bitcast(I32)
+            )
+            table.append(words)
+
         load_table(0)
         b_rows = keep.tile([P, DEAL * P], F32, name="b_rows")
         nc.gpsimd.memset(b_rows[:], 0.0)
@@ -114,49 +117,63 @@ def tile_list_tabres_gelu_kernel(
         bias = keep.tile([P, HALVES, DEAL], F32, name="bias")
         nc.scalar.copy(out=bias[:], in_=b_bank[:, :, GROUP : GROUP + HALVES].rearrange("p u g -> p g u"))
 
+        w4 = []
+        for g in range(HALVES):
+            words = keep.tile([P, PASSES, 2 * HALF], U8, name="w4_%d" % g, align_bytes=ALIGN)
+            nc.scalar.copy(
+                out=words[:].bitcast(U16).rearrange("p a (u m) -> p u a m", u=DEAL),
+                in_=w4_raw[:].bitcast(U16)[:, :, g * HALF : (g + 1) * HALF].rearrange("p a (m u) -> p u a m", u=DEAL),
+            )
+            w4.append(words)
+
         picked = keep.tile([P, S], U8, name="picked", align_bytes=BURST)
         nc.vector.tensor_copy(out=picked[:], in_=window[:].indirect(offsets[:]))
-
-        def move_plane(a):
+        for a in range(PASSES):
+            queue = nc.sync if a == 0 else nc.gpsimd
             for r in range(PLANE_ROWS):
                 first = QUAD + a + PLANE_ROWS * r
-                nc.sync.dma_start(
+                queue.dma_start(
                     out=v_planes[a][r:P:QUAD, :].bitcast(I32),
                     in_=picked[first : 3 * QUAD : PLANE_ROWS * PLANE_ROWS, :].bitcast(I32),
                 )
 
-        for a in range(PASSES):
-            move_plane(a)
-            if a + 1 < PASSES:
-                load_table(a + 1)
-
-        v_codes = []
-        for a in range(PASSES):
-            codes = keep.tile([P, S], U32, name="v_codes%d" % a, align_bytes=ALIGN)
-            if a < PASSES - 1:
-                nc.vector.tensor_copy(out=codes[:], in_=table[a][:].indirect(offsets[:]))
-            else:
-                for s in range(SLICES):
-                    nc.vector.tensor_copy(out=codes[:, token_cols(s)], in_=table[a][:].indirect(entries(s)))
-            v_codes.append(codes)
-
-        def staging(name, shape):
-            return stage.tile(shape, BF16, name=name, tag="staging", align_bytes=ALIGN)
+        for a in range(1, PASSES):
+            load_table(a)
 
         down_codes = []
         down_planes = []
-
-        def quantise_down(a):
-            grouped = staging("down_bf%d" % a, [P, R * PACK])
+        for a in range(PASSES):
+            grouped = placed(results_at(0) + a * STAGE, [P, R * PACK], BF16, "down_bf%d" % a)
             nc.scalar.copy(
                 out=grouped[:].rearrange("p (t m j) -> p m t j", t=PACK, j=PACK),
-                in_=down_raw[a][:].rearrange("p j (m t) -> p m t j", t=PACK),
+                in_=down_raw[:, a, :].rearrange("p (j m t) -> p m t j", j=PACK, t=PACK),
             )
             codes = keep.tile([P, R], U32, name="down_codes%d" % a, align_bytes=ALIGN)
             plane = keep.tile([P, R], U8, name="down_plane%d" % a, align_bytes=ALIGN)
             nc.vector.quantize_mx(out=codes[:].bitcast(FP8X4), scales=plane[:], in_=grouped[:])
             down_codes.append(codes)
             down_planes.append(plane)
+
+        up_raw = placed(results_at(1), [P, PACK, M], F32, "up_raw")
+        nc.sync.dma_start(out=up_raw[:], in_=up.rearrange("(p j) n -> p j n", j=PACK))
+
+        last = PASSES - 1
+        v_codes = []
+        w4_plane = []
+        for a in range(PASSES):
+            codes = keep.tile([P, S], U32, name="v_codes%d" % a, align_bytes=ALIGN)
+            v_codes.append(codes)
+            if a < last:
+                nc.vector.tensor_copy(out=codes[:], in_=table[a][:].indirect(offsets[:]))
+                plane = placed(region(a + 1) - NICHE, [P, PASSES, HALF], U8, "w4_plane%d" % a)
+                nc.vector.tensor_copy(
+                    out=plane[:].rearrange("p a (u m) -> p u a m", u=DEAL),
+                    in_=w4_plane_raw[:, :, a * HALF : (a + 1) * HALF].rearrange("p a (m u) -> p u a m", u=DEAL),
+                )
+                w4_plane.append(plane)
+            else:
+                for s in range(SLICES):
+                    nc.vector.tensor_copy(out=codes[:, token_cols(s)], in_=table[a][:].indirect(entries(s)))
 
         def h_pass(sums, t, a, cols, start, stop):
             nc.tensor.matmul_mx(
@@ -169,8 +186,8 @@ def tile_list_tabres_gelu_kernel(
                 stop=stop,
             )
 
-        last = PASSES - 1
-        chunks = [psum.tile([P, PACK, P], F32, name="h_chunk%d" % c, tag="bank") for c in range(BANKS)]
+        chunks = [psum.tile([P, PACK, P], F32, name="h_chunk%d" % c, tag="bank") for c in range(BANK // P)]
+        wide = [psum.tile([P, BANK], F32, name="h_wide%d" % t, tag="bank") for t in range(PACK)]
 
         def chunk_pass(c, a):
             for t in range(PACK):
@@ -178,42 +195,25 @@ def tile_list_tabres_gelu_kernel(
                     chunks[c][:, t, :], t, a, slice(c * P, (c + 1) * P), a == 0 and t == 0, a == last and t == PACK - 1
                 )
 
-        for a in range(PASSES):
-            quantise_down(a)
-            if a < last:
-                for c in range(BANKS):
-                    chunk_pass(c, a)
+        for a in range(last):
+            for c in range(BANK // P):
+                chunk_pass(c, a)
+            for t in range(PACK):
+                h_pass(wide[t][:], t, a, token_cols(1), a == 0, False)
 
-        up_raw = tenant(3, [P, PACK, M], F32, "up_raw")
-        nc.sync.dma_start(out=up_raw[:], in_=up.rearrange("(p j) n -> p j n", j=PACK))
-        w4_raw = tenant(4, [P, PASSES, 2 * M], U8, "w4_raw")
-        nc.sync.dma_start(out=w4_raw[:].bitcast(I32), in_=w4_words.rearrange("a p n -> p a n").bitcast(I32))
+        def scalar_copy(out, in_):
+            nc.scalar.copy(out=out, in_=in_)
 
-        w4 = []
-        w4_plane = []
-
-        def deal_w4(g):
-            words = keep.tile([P, PASSES, 2 * HALF], U8, name="w4_%d" % g, align_bytes=ALIGN)
-            plane = keep.tile([P, PASSES, HALF], U8, name="w4_plane%d" % g, align_bytes=ALIGN)
-            nc.vector.tensor_copy(
-                out=plane[:].rearrange("p a (u m) -> p u a m", u=DEAL),
-                in_=w4_plane_raw[:, :, g * HALF : (g + 1) * HALF].rearrange("p a (m u) -> p u a m", u=DEAL),
-            )
-            nc.vector.tensor_copy(
-                out=words[:].bitcast(U16).rearrange("p a (u m) -> p u a m", u=DEAL),
-                in_=w4_raw[:].bitcast(U16)[:, :, g * HALF : (g + 1) * HALF].rearrange("p a (m u) -> p u a m", u=DEAL),
-            )
-            w4.append(words)
-            w4_plane.append(plane)
+        def vector_copy(out, in_):
+            nc.vector.tensor_copy(out=out, in_=in_)
 
         up_codes = []
         up_planes = []
 
-        def quantise_up(g):
-            grouped = staging("up_bf%d" % g, [P, HALF * PACK])
-            nc.scalar.copy(
-                out=grouped[:].rearrange("p (u m j) -> p m u j", u=DEAL, j=PACK),
-                in_=up_raw[:, :, g * HALF : (g + 1) * HALF].rearrange("p j (m u) -> p m u j", u=DEAL),
+        def quantise_up(copy, g, grouped):
+            copy(
+                grouped[:].rearrange("p (u m j) -> p m u j", u=DEAL, j=PACK),
+                up_raw[:, :, g * HALF : (g + 1) * HALF].rearrange("p j (m u) -> p m u j", u=DEAL),
             )
             codes = keep.tile([P, HALF], U32, name="up_codes%d" % g, align_bytes=ALIGN)
             plane = keep.tile([P, HALF], U8, name="up_plane%d" % g, align_bytes=ALIGN)
@@ -225,20 +225,25 @@ def tile_list_tabres_gelu_kernel(
         h_plane = keep.tile([P, S], U8, name="h_plane", align_bytes=ALIGN)
         for s in range(SLICES):
             cols = token_cols(s)
-            grouped = staging("h_bf%d" % s, [P, BANK * PACK])
-            if s < EARLY_SLICES:
+            n, place = divmod(2 * s, REGION // STAGE)
+            grouped = staging(3 + n, place + 1, "h_bf%d" % s, [P, BANK * PACK])
+            if s == 0:
                 for c in range(BANK // P):
-                    chunk_pass(s * BANK // P + c, last)
+                    chunk_pass(c, last)
                     nc.scalar.copy(
                         out=grouped[:, c * P * PACK : (c + 1) * P * PACK].rearrange("p (n t) -> p n t", t=PACK),
-                        in_=chunks[s * BANK // P + c][:].rearrange("p t n -> p n t"),
+                        in_=chunks[c][:].rearrange("p t n -> p n t"),
                     )
             else:
-                apart = staging("h_apart", [P, PACK, BANK])
+                apart = staging(3 + n, place, "h_apart%d" % s, [P, PACK, BANK])
                 for t in range(PACK):
-                    bank = psum.tile([P, BANK], F32, name="h_late", tag="bank")
-                    for a in range(PASSES):
-                        h_pass(bank[:], t, a, cols, a == 0, a == last)
+                    if s < EARLY_SLICES:
+                        bank = wide[t]
+                        h_pass(bank[:], t, last, cols, False, True)
+                    else:
+                        bank = psum.tile([P, BANK], F32, name="h_late", tag="bank")
+                        for a in range(PASSES):
+                            h_pass(bank[:], t, a, cols, a == 0, a == last)
                     nc.scalar.copy(out=apart[:, t, :], in_=bank[:])
                 nc.vector.tensor_copy(
                     out=grouped[:].rearrange("p (c i t) -> p c t i", i=LINE, t=PACK),
@@ -246,23 +251,20 @@ def tile_list_tabres_gelu_kernel(
                 )
             nc.vector.quantize_mx(out=h_codes[:, cols].bitcast(FP8X4), scales=h_plane[:, cols], in_=grouped[:])
             if s == 0:
-                quantise_up(0)
-                deal_w4(0)
+                quantise_up(vector_copy, 0, staging(3, 0, "up_bf0", [P, HALF * PACK]))
 
         resid = []
 
         def load_resid(i):
-            rows = tenant((0, 1, 2, 4, 3)[i % 5], [P, T], F32, "resid%d" % i)
+            rows = placed(region(i % REGIONS), [P, T], F32, "resid%d" % i)
             g, u = divmod(i, DEAL)
-            nc.sync.dma_start(out=rows[:], in_=rT[g * DEAL * P + u : (g + 1) * DEAL * P : DEAL, :])
+            nc.sync.dma_start(out=rows[:], in_=rT[g * HALF + u : (g + 1) * HALF : DEAL, :])
             resid.append(rows)
 
-        deal_w4(1)
-        quantise_up(1)
-        for i in range(5):
+        for i in range(REGIONS):
             load_resid(i)
 
-        results = [keep.tile([P, DEAL, S], F32, name="results%d" % g, align_bytes=BURST) for g in range(HALVES)]
+        results = []
 
         def store(g, first, end):
             dealt = out[g * HALF : (g + 1) * HALF, :].rearrange("(p u) s -> p (u s)", u=DEAL)
@@ -273,8 +275,10 @@ def tile_list_tabres_gelu_kernel(
 
         for i in range(TILES):
             g, u = divmod(i, DEAL)
+            if u == 0:
+                results.append(placed(results_at(g), [P, DEAL, S], F32, "results%d" % g))
             rows = slice(u * P, (u + 1) * P)
-            act = acts.tile([P, S], F32, name="act")
+            act = acts.tile([P, S], F32, name="act", tag="act", align_bytes=ALIGN)
             result = results[g][:, u, :]
             for s in range(SLICES):
                 cols = token_cols(s)
@@ -305,8 +309,11 @@ def tile_list_tabres_gelu_kernel(
                     )
             if i > 0:
                 nc.vector.tensor_tensor(out=result, in0=resid[i][:].indirect(offsets[:]), in1=act[:], op=ADD)
-            if i + 5 < TILES:
-                load_resid(i + 5)
+            if i == ACT_BUFS - 1:
+                up_late = acts.tile([P, HALF * PACK], BF16, name="up_bf1", tag="act", align_bytes=ALIGN)
+                quantise_up(scalar_copy, 1, up_late)
+            if i + REGIONS < TILES:
+                load_resid(i + REGIONS)
             if i == DEAL - 1:
                 store(0, 0, DEAL)
             if i == TILES - 2:

@@ -39,8 +39,10 @@ RESULTS = 4 * DEAL * S
 STAGE = 2 * PACK * BANK
 REGIONS = 5
 NICHE = PASSES * HALF
+RESID_REGIONS = (0, 2, 3, 4, 1)
 EARLY_SLICES = BANKS // PACK
 ACT_BUFS = 3
+WARM_COLS = 8
 
 
 def tile_list_tabres_gelu_kernel(
@@ -57,13 +59,14 @@ def tile_list_tabres_gelu_kernel(
             return big.tile(shape, dtype, name=name, align_bytes=BURST, offset=offset)
 
         def region(n):
-            return n * REGION + min(n, 2) * NICHE
+            return n * REGION + (NICHE if n < 3 else 2 * NICHE)
 
         def results_at(g):
             return region(REGIONS) + g * RESULTS
 
-        def staging(n, place, name, shape):
-            return placed(region(n) + place * STAGE, shape, BF16, name)
+        def staging(place, name, shape):
+            start = results_at(0) if place < 2 * EARLY_SLICES else region(1) - 2 * EARLY_SLICES * STAGE
+            return placed(start + place * STAGE, shape, BF16, name)
 
         def token_cols(s):
             return slice(s * BANK, (s + 1) * BANK)
@@ -73,7 +76,7 @@ def tile_list_tabres_gelu_kernel(
         def entries(s):
             return offsets[:, s * BANK // GROUP : (s + 1) * BANK // GROUP]
 
-        window = placed(region(2) - T // 2, [P, T], U8, "window")
+        window = placed(region(3) - T, [P, T], U8, "window")
         w4_plane_raw = keep.tile([P, PASSES, M], U8, name="w4_plane_raw", align_bytes=BURST)
         v_planes = [keep.tile([P, S], U8, name="v_plane%d" % a, align_bytes=BURST) for a in range(PASSES)]
         nc.vector.memset(window[:].bitcast(I32), 0)
@@ -93,7 +96,7 @@ def tile_list_tabres_gelu_kernel(
         table = []
 
         def load_table(a):
-            words = placed(region(a) + (NICHE if a < HALVES else 0), [P, T], U32, "table%d" % a)
+            words = placed((0, region(3) - REGION, region(3) + REGION // 2)[a], [P, T], U32, "table%d" % a)
             nc.sync.dma_start(
                 out=words[:].bitcast(I32), in_=tab_words[a].rearrange("p t i -> p (t i)").bitcast(I32)
             )
@@ -117,6 +120,9 @@ def tile_list_tabres_gelu_kernel(
         bias = keep.tile([P, HALVES, DEAL], F32, name="bias")
         nc.scalar.copy(out=bias[:], in_=b_bank[:, :, GROUP : GROUP + HALVES].rearrange("p u g -> p g u"))
 
+        warm = keep.tile([P, WARM_COLS], F32, name="warm")
+        nc.scalar.activation(out=warm[:], in_=ident[:, 0:WARM_COLS], func=GELU)
+
         w4 = []
         for g in range(HALVES):
             words = keep.tile([P, PASSES, 2 * HALF], U8, name="w4_%d" % g, align_bytes=ALIGN)
@@ -137,13 +143,13 @@ def tile_list_tabres_gelu_kernel(
                     in_=picked[first : 3 * QUAD : PLANE_ROWS * PLANE_ROWS, :].bitcast(I32),
                 )
 
-        for a in range(1, PASSES):
-            load_table(a)
+        load_table(1)
 
         down_codes = []
         down_planes = []
         for a in range(PASSES):
-            grouped = placed(results_at(0) + a * STAGE, [P, R * PACK], BF16, "down_bf%d" % a)
+            start = region(4) if a == 0 else results_at(0) + a * STAGE
+            grouped = placed(start, [P, R * PACK], BF16, "down_bf%d" % a)
             nc.scalar.copy(
                 out=grouped[:].rearrange("p (t m j) -> p m t j", t=PACK, j=PACK),
                 in_=down_raw[:, a, :].rearrange("p (j m t) -> p m t j", j=PACK, t=PACK),
@@ -154,6 +160,7 @@ def tile_list_tabres_gelu_kernel(
             down_codes.append(codes)
             down_planes.append(plane)
 
+        load_table(2)
         up_raw = placed(results_at(1), [P, PACK, M], F32, "up_raw")
         nc.sync.dma_start(out=up_raw[:], in_=up.rearrange("(p j) n -> p j n", j=PACK))
 
@@ -165,7 +172,7 @@ def tile_list_tabres_gelu_kernel(
             v_codes.append(codes)
             if a < last:
                 nc.vector.tensor_copy(out=codes[:], in_=table[a][:].indirect(offsets[:]))
-                plane = placed(region(a + 1) - NICHE, [P, PASSES, HALF], U8, "w4_plane%d" % a)
+                plane = placed((0, region(3) - NICHE)[a], [P, PASSES, HALF], U8, "w4_plane%d" % a)
                 nc.vector.tensor_copy(
                     out=plane[:].rearrange("p a (u m) -> p u a m", u=DEAL),
                     in_=w4_plane_raw[:, :, a * HALF : (a + 1) * HALF].rearrange("p a (m u) -> p u a m", u=DEAL),
@@ -225,8 +232,7 @@ def tile_list_tabres_gelu_kernel(
         h_plane = keep.tile([P, S], U8, name="h_plane", align_bytes=ALIGN)
         for s in range(SLICES):
             cols = token_cols(s)
-            n, place = divmod(2 * s, REGION // STAGE)
-            grouped = staging(3 + n, place + 1, "h_bf%d" % s, [P, BANK * PACK])
+            grouped = staging(2 * s + 1, "h_bf%d" % s, [P, BANK * PACK])
             if s == 0:
                 for c in range(BANK // P):
                     chunk_pass(c, last)
@@ -235,7 +241,7 @@ def tile_list_tabres_gelu_kernel(
                         in_=chunks[c][:].rearrange("p t n -> p n t"),
                     )
             else:
-                apart = staging(3 + n, place, "h_apart%d" % s, [P, PACK, BANK])
+                apart = staging(2 * s, "h_apart%d" % s, [P, PACK, BANK])
                 for t in range(PACK):
                     if s < EARLY_SLICES:
                         bank = wide[t]
@@ -251,14 +257,15 @@ def tile_list_tabres_gelu_kernel(
                 )
             nc.vector.quantize_mx(out=h_codes[:, cols].bitcast(FP8X4), scales=h_plane[:, cols], in_=grouped[:])
             if s == 0:
-                quantise_up(vector_copy, 0, staging(3, 0, "up_bf0", [P, HALF * PACK]))
+                quantise_up(vector_copy, 0, staging(0, "up_bf0", [P, HALF * PACK]))
 
         resid = []
 
         def load_resid(i):
-            rows = placed(region(i % REGIONS), [P, T], F32, "resid%d" % i)
+            rows = placed(region(RESID_REGIONS[i % REGIONS]), [P, T], F32, "resid%d" % i)
             g, u = divmod(i, DEAL)
-            nc.sync.dma_start(out=rows[:], in_=rT[g * HALF + u : (g + 1) * HALF : DEAL, :])
+            queue = nc.sync if i % 2 or i == 0 else nc.gpsimd
+            queue.dma_start(out=rows[:], in_=rT[g * HALF + u : (g + 1) * HALF : DEAL, :])
             resid.append(rows)
 
         for i in range(REGIONS):
@@ -266,9 +273,9 @@ def tile_list_tabres_gelu_kernel(
 
         results = []
 
-        def store(g, first, end):
+        def store(queue, g, first, end):
             dealt = out[g * HALF : (g + 1) * HALF, :].rearrange("(p u) s -> p (u s)", u=DEAL)
-            nc.sync.dma_start(
+            queue.dma_start(
                 out=dealt[:, first * S : end * S],
                 in_=results[g][:].rearrange("p u s -> p (u s)")[:, first * S : end * S],
             )
@@ -309,13 +316,13 @@ def tile_list_tabres_gelu_kernel(
                     )
             if i > 0:
                 nc.vector.tensor_tensor(out=result, in0=resid[i][:].indirect(offsets[:]), in1=act[:], op=ADD)
+            if i + REGIONS < TILES:
+                load_resid(i + REGIONS)
             if i == ACT_BUFS - 1:
                 up_late = acts.tile([P, HALF * PACK], BF16, name="up_bf1", tag="act", align_bytes=ALIGN)
                 quantise_up(scalar_copy, 1, up_late)
-            if i + REGIONS < TILES:
-                load_resid(i + REGIONS)
             if i == DEAL - 1:
-                store(0, 0, DEAL)
+                store(nc.gpsimd, 0, 0, DEAL)
             if i == TILES - 2:
-                store(1, 0, DEAL - 1)
-        store(1, DEAL - 1, DEAL)
+                store(nc.sync, 1, 0, DEAL - 1)
+        store(nc.sync, 1, DEAL - 1, DEAL)

@@ -42,7 +42,6 @@ NICHE = PASSES * HALF
 RESID_REGIONS = (0, 2, 3, 4, 1)
 EARLY_SLICES = BANKS // PACK
 ACT_BUFS = 3
-WARM_COLS = 8
 
 
 def tile_list_tabres_gelu_kernel(
@@ -119,9 +118,6 @@ def tile_list_tabres_gelu_kernel(
             nc.tensor.transpose(b_bank[:, u, :], b_rows[:, u::DEAL], ident[:])
         bias = keep.tile([P, HALVES, DEAL], F32, name="bias")
         nc.scalar.copy(out=bias[:], in_=b_bank[:, :, GROUP : GROUP + HALVES].rearrange("p u g -> p g u"))
-
-        warm = keep.tile([P, WARM_COLS], F32, name="warm")
-        nc.scalar.activation(out=warm[:], in_=ident[:, 0:WARM_COLS], func=GELU)
 
         w4 = []
         for g in range(HALVES):

@@ -37,9 +37,9 @@ ALIGN = 64
 REGION = 4 * T
 RESULTS = 4 * DEAL * S
 STAGE = 2 * PACK * BANK
-REGIONS = 5
-NICHE = PASSES * HALF
-RESID_REGIONS = (0, 2, 3, 4, 1)
+REGIONS = 7
+UP_REGION = PASSES
+RESID_REGIONS = (4, 2, 5, 1, 6, 0, 3, 4)
 EARLY_SLICES = BANKS // PACK
 ACT_BUFS = 3
 
@@ -58,14 +58,10 @@ def tile_list_tabres_gelu_kernel(
             return big.tile(shape, dtype, name=name, align_bytes=BURST, offset=offset)
 
         def region(n):
-            return n * REGION + (NICHE if n < 3 else 2 * NICHE)
+            return n * REGION
 
         def results_at(g):
             return region(REGIONS) + g * RESULTS
-
-        def staging(place, name, shape):
-            start = results_at(0) if place < 2 * EARLY_SLICES else region(1) - 2 * EARLY_SLICES * STAGE
-            return placed(start + place * STAGE, shape, BF16, name)
 
         def token_cols(s):
             return slice(s * BANK, (s + 1) * BANK)
@@ -75,7 +71,31 @@ def tile_list_tabres_gelu_kernel(
         def entries(s):
             return offsets[:, s * BANK // GROUP : (s + 1) * BANK // GROUP]
 
-        window = placed(region(3) - T, [P, T], U8, "window")
+        down_raw = placed(results_at(1), [P, PASSES, PACK * R], F32, "down_raw")
+        nc.gpsimd.dma_start(out=down_raw[:], in_=down.rearrange("(a p j) r -> p a (j r)", p=P, j=PACK))
+        table = []
+        for a in range(PASSES):
+            words = placed(region(a), [P, T], U32, "table%d" % a)
+            nc.gpsimd.dma_start(
+                out=words[:].bitcast(I32), in_=tab_words[a].rearrange("p t i -> p (t i)").bitcast(I32)
+            )
+            table.append(words)
+        up_raw = placed(region(UP_REGION), [P, PACK, M], F32, "up_raw")
+        nc.gpsimd.dma_start(out=up_raw[:], in_=up.rearrange("(p j) n -> p j n", j=PACK))
+
+        resid = {}
+
+        def load_resid(i):
+            rows = placed(region(RESID_REGIONS[i]), [P, T], F32, "resid%d" % i)
+            g, u = divmod(i, DEAL)
+            queue = nc.sync if i % 2 else nc.gpsimd
+            queue.dma_start(out=rows[:], in_=rT[g * HALF + u : (g + 1) * HALF : DEAL, :])
+            resid[i] = rows
+
+        for i in (0, 2, 4):
+            load_resid(i)
+
+        window = placed(results_at(0) + PASSES * STAGE + PASSES * 2 * M, [P, T], U8, "window")
         w4_plane_raw = keep.tile([P, PASSES, M], U8, name="w4_plane_raw", align_bytes=BURST)
         v_planes = [keep.tile([P, S], U8, name="v_plane%d" % a, align_bytes=BURST) for a in range(PASSES)]
         nc.vector.memset(window[:].bitcast(I32), 0)
@@ -90,27 +110,15 @@ def tile_list_tabres_gelu_kernel(
             nc.sync.dma_start(
                 out=window[QUAD + c : 3 * QUAD : PLANE_ROWS, :].bitcast(I32), in_=tab_scales[c].bitcast(I32)
             )
-        down_raw = placed(results_at(1), [P, PASSES, PACK * R], F32, "down_raw")
-        nc.sync.dma_start(out=down_raw[:], in_=down.rearrange("(a p j) r -> p a (j r)", p=P, j=PACK))
-        table = []
-
-        def load_table(a):
-            words = placed((0, region(3) - REGION, region(3) + REGION // 2)[a], [P, T], U32, "table%d" % a)
-            nc.sync.dma_start(
-                out=words[:].bitcast(I32), in_=tab_words[a].rearrange("p t i -> p (t i)").bitcast(I32)
-            )
-            table.append(words)
-
-        load_table(0)
-        b_rows = keep.tile([P, DEAL * P], F32, name="b_rows")
-        nc.gpsimd.memset(b_rows[:], 0.0)
-        nc.scalar.dma_start(out=b_rows[GROUP : GROUP + HALVES, :], in_=b.rearrange("(g c) -> g c", g=HALVES))
         for r in range(PLANE_ROWS):
-            nc.gpsimd.dma_start(
+            nc.sync.dma_start(
                 out=w4_plane_raw[r:P:QUAD, :, :].bitcast(I32),
                 in_=w4_scales[:, r::PLANE_ROWS, :].rearrange("a q n -> q a n").bitcast(I32),
             )
 
+        b_rows = placed(results_at(1) - 4 * DEAL * P, [P, DEAL * P], F32, "b_rows")
+        nc.vector.memset(b_rows[:], 0.0)
+        nc.scalar.dma_start(out=b_rows[GROUP : GROUP + HALVES, :], in_=b.rearrange("(g c) -> g c", g=HALVES))
         ident = keep.tile([P, P], F32, name="ident")
         make_identity(nc, ident[:])
         b_bank = psum.tile([P, DEAL, P], F32, name="b_bank", tag="bank")
@@ -131,21 +139,26 @@ def tile_list_tabres_gelu_kernel(
         picked = keep.tile([P, S], U8, name="picked", align_bytes=BURST)
         nc.vector.tensor_copy(out=picked[:], in_=window[:].indirect(offsets[:]))
         for a in range(PASSES):
-            queue = nc.sync if a == 0 else nc.gpsimd
             for r in range(PLANE_ROWS):
                 first = QUAD + a + PLANE_ROWS * r
-                queue.dma_start(
+                nc.sync.dma_start(
                     out=v_planes[a][r:P:QUAD, :].bitcast(I32),
                     in_=picked[first : 3 * QUAD : PLANE_ROWS * PLANE_ROWS, :].bitcast(I32),
                 )
 
-        load_table(1)
+        w4_plane = []
+        for g in range(HALVES):
+            plane = keep.tile([P, PASSES, HALF], U8, name="w4_plane%d" % g, align_bytes=ALIGN)
+            nc.vector.tensor_copy(
+                out=plane[:].rearrange("p a (u m) -> p u a m", u=DEAL),
+                in_=w4_plane_raw[:, :, g * HALF : (g + 1) * HALF].rearrange("p a (m u) -> p u a m", u=DEAL),
+            )
+            w4_plane.append(plane)
 
         down_codes = []
         down_planes = []
         for a in range(PASSES):
-            start = region(4) if a == 0 else results_at(0) + a * STAGE
-            grouped = placed(start, [P, R * PACK], BF16, "down_bf%d" % a)
+            grouped = placed(results_at(0) + a * STAGE, [P, R * PACK], BF16, "down_bf%d" % a)
             nc.scalar.copy(
                 out=grouped[:].rearrange("p (t m j) -> p m t j", t=PACK, j=PACK),
                 in_=down_raw[:, a, :].rearrange("p (j m t) -> p m t j", j=PACK, t=PACK),
@@ -156,24 +169,13 @@ def tile_list_tabres_gelu_kernel(
             down_codes.append(codes)
             down_planes.append(plane)
 
-        load_table(2)
-        up_raw = placed(results_at(1), [P, PACK, M], F32, "up_raw")
-        nc.sync.dma_start(out=up_raw[:], in_=up.rearrange("(p j) n -> p j n", j=PACK))
-
         last = PASSES - 1
         v_codes = []
-        w4_plane = []
         for a in range(PASSES):
             codes = keep.tile([P, S], U32, name="v_codes%d" % a, align_bytes=ALIGN)
             v_codes.append(codes)
             if a < last:
                 nc.vector.tensor_copy(out=codes[:], in_=table[a][:].indirect(offsets[:]))
-                plane = placed((0, region(3) - NICHE)[a], [P, PASSES, HALF], U8, "w4_plane%d" % a)
-                nc.vector.tensor_copy(
-                    out=plane[:].rearrange("p a (u m) -> p u a m", u=DEAL),
-                    in_=w4_plane_raw[:, :, a * HALF : (a + 1) * HALF].rearrange("p a (m u) -> p u a m", u=DEAL),
-                )
-                w4_plane.append(plane)
             else:
                 for s in range(SLICES):
                     nc.vector.tensor_copy(out=codes[:, token_cols(s)], in_=table[a][:].indirect(entries(s)))
@@ -228,7 +230,8 @@ def tile_list_tabres_gelu_kernel(
         h_plane = keep.tile([P, S], U8, name="h_plane", align_bytes=ALIGN)
         for s in range(SLICES):
             cols = token_cols(s)
-            grouped = staging(2 * s + 1, "h_bf%d" % s, [P, BANK * PACK])
+            stage_at = (region(1), region(0), results_at(1))[s]
+            grouped = placed(stage_at, [P, BANK * PACK], BF16, "h_bf%d" % s)
             if s == 0:
                 for c in range(BANK // P):
                     chunk_pass(c, last)
@@ -237,7 +240,7 @@ def tile_list_tabres_gelu_kernel(
                         in_=chunks[c][:].rearrange("p t n -> p n t"),
                     )
             else:
-                apart = staging(2 * s, "h_apart%d" % s, [P, PACK, BANK])
+                apart = placed(stage_at + STAGE, [P, PACK, BANK], BF16, "h_apart%d" % s)
                 for t in range(PACK):
                     if s < EARLY_SLICES:
                         bank = wide[t]
@@ -253,18 +256,9 @@ def tile_list_tabres_gelu_kernel(
                 )
             nc.vector.quantize_mx(out=h_codes[:, cols].bitcast(FP8X4), scales=h_plane[:, cols], in_=grouped[:])
             if s == 0:
-                quantise_up(vector_copy, 0, staging(0, "up_bf0", [P, HALF * PACK]))
+                quantise_up(vector_copy, 0, placed(results_at(1) + 2 * STAGE, [P, HALF * PACK], BF16, "up_bf0"))
 
-        resid = []
-
-        def load_resid(i):
-            rows = placed(region(RESID_REGIONS[i % REGIONS]), [P, T], F32, "resid%d" % i)
-            g, u = divmod(i, DEAL)
-            queue = nc.sync if i % 2 or i == 0 else nc.gpsimd
-            queue.dma_start(out=rows[:], in_=rT[g * HALF + u : (g + 1) * HALF : DEAL, :])
-            resid.append(rows)
-
-        for i in range(REGIONS):
+        for i in (1, 3, 5):
             load_resid(i)
 
         results = []
@@ -312,11 +306,12 @@ def tile_list_tabres_gelu_kernel(
                     )
             if i > 0:
                 nc.vector.tensor_tensor(out=result, in0=resid[i][:].indirect(offsets[:]), in1=act[:], op=ADD)
-            if i + REGIONS < TILES:
-                load_resid(i + REGIONS)
+            if i == 0:
+                load_resid(TILES - 1)
             if i == ACT_BUFS - 1:
                 up_late = acts.tile([P, HALF * PACK], BF16, name="up_bf1", tag="act", align_bytes=ALIGN)
                 quantise_up(scalar_copy, 1, up_late)
+                load_resid(TILES - 2)
             if i == DEAL - 1:
                 store(nc.gpsimd, 0, 0, DEAL)
             if i == TILES - 2:

@@ -71,8 +71,16 @@ def tile_list_tabres_gelu_kernel(
         def entries(s):
             return offsets[:, s * BANK // GROUP : (s + 1) * BANK // GROUP]
 
-        down_raw = placed(results_at(1), [P, PASSES, PACK * R], F32, "down_raw")
-        nc.gpsimd.dma_start(out=down_raw[:], in_=down.rearrange("(a p j) r -> p a (j r)", p=P, j=PACK))
+        down_raw = []
+        for a in range(PASSES):
+            rows = placed(results_at(1) + a * 4 * PACK * R, [P, PACK * R], F32, "down_raw%d" % a)
+            nc.gpsimd.dma_start(
+                out=rows[:], in_=down[a * K_PASS : (a + 1) * K_PASS, :].rearrange("(p j) r -> p (j r)", j=PACK)
+            )
+            down_raw.append(rows)
+            if a == 0:
+                ident = keep.tile([P, P], F32, name="ident")
+                make_identity(nc, ident[:])
         table = []
         for a in range(PASSES):
             words = placed(region(a), [P, T], U32, "table%d" % a)
@@ -98,10 +106,15 @@ def tile_list_tabres_gelu_kernel(
         window = placed(results_at(0) + PASSES * STAGE + PASSES * 2 * M, [P, T], U8, "window")
         w4_plane_raw = keep.tile([P, PASSES, M], U8, name="w4_plane_raw", align_bytes=BURST)
         v_planes = [keep.tile([P, S], U8, name="v_plane%d" % a, align_bytes=BURST) for a in range(PASSES)]
-        nc.vector.memset(window[:].bitcast(I32), 0)
-        nc.vector.memset(w4_plane_raw[:].bitcast(I32), 0)
+
+        def clear(words):
+            nc.vector.memset(words[:, :1], 0)
+            nc.vector.memset(words[:, 1:], 0)
+
+        clear(window[:].bitcast(I32))
+        clear(w4_plane_raw[:].rearrange("p a n -> p (a n)").bitcast(I32))
         for plane in v_planes:
-            nc.vector.memset(plane[:].bitcast(I32), 0)
+            clear(plane[:].bitcast(I32))
 
         w4_raw = placed(results_at(0) + PASSES * STAGE, [P, PASSES, 2 * M], U8, "w4_raw")
         nc.sync.dma_start(out=w4_raw[:].bitcast(I32), in_=w4_words.rearrange("a p n -> p a n").bitcast(I32))
@@ -117,10 +130,8 @@ def tile_list_tabres_gelu_kernel(
             )
 
         b_rows = placed(results_at(1) - 4 * DEAL * P, [P, DEAL * P], F32, "b_rows")
-        nc.vector.memset(b_rows[:], 0.0)
+        clear(b_rows[:])
         nc.scalar.dma_start(out=b_rows[GROUP : GROUP + HALVES, :], in_=b.rearrange("(g c) -> g c", g=HALVES))
-        ident = keep.tile([P, P], F32, name="ident")
-        make_identity(nc, ident[:])
         b_bank = psum.tile([P, DEAL, P], F32, name="b_bank", tag="bank")
         for u in range(DEAL):
             nc.tensor.transpose(b_bank[:, u, :], b_rows[:, u::DEAL], ident[:])
@@ -161,7 +172,7 @@ def tile_list_tabres_gelu_kernel(
             grouped = placed(results_at(0) + a * STAGE, [P, R * PACK], BF16, "down_bf%d" % a)
             nc.scalar.copy(
                 out=grouped[:].rearrange("p (t m j) -> p m t j", t=PACK, j=PACK),
-                in_=down_raw[:, a, :].rearrange("p (j m t) -> p m t j", j=PACK, t=PACK),
+                in_=down_raw[a][:].rearrange("p (j m t) -> p m t j", j=PACK, t=PACK),
             )
             codes = keep.tile([P, R], U32, name="down_codes%d" % a, align_bytes=ALIGN)
             plane = keep.tile([P, R], U8, name="down_plane%d" % a, align_bytes=ALIGN)

@@ -28,7 +28,6 @@ TILES = M // P
 QUAD = 32
 PLANE_ROWS = 4
 GROUP = 16
-LINE = 4
 DEAL = 4
 HALVES = TILES // DEAL
 HALF = M // HALVES
@@ -39,7 +38,7 @@ RESULTS = 4 * DEAL * S
 STAGE = 2 * PACK * BANK
 REGIONS = 7
 UP_REGION = PASSES
-RESID_REGIONS = (4, 2, 5, 1, 6, 0, 3, 4)
+RESID_REGIONS = (4, 5, 6, 0, 1, 2, 4, 3)
 EARLY_SLICES = BANKS // PACK
 ACT_BUFS = 3
 
@@ -96,11 +95,10 @@ def tile_list_tabres_gelu_kernel(
         def load_resid(i):
             rows = placed(region(RESID_REGIONS[i]), [P, T], F32, "resid%d" % i)
             g, u = divmod(i, DEAL)
-            queue = nc.sync if i % 2 else nc.gpsimd
-            queue.dma_start(out=rows[:], in_=rT[g * HALF + u : (g + 1) * HALF : DEAL, :])
+            nc.gpsimd.dma_start(out=rows[:], in_=rT[g * HALF + u : (g + 1) * HALF : DEAL, :])
             resid[i] = rows
 
-        for i in (0, 2, 4):
+        for i in (0, 1, 2):
             load_resid(i)
 
         window = placed(results_at(0) + PASSES * STAGE + PASSES * 2 * M, [P, T], U8, "window")
@@ -202,20 +200,18 @@ def tile_list_tabres_gelu_kernel(
                 stop=stop,
             )
 
-        chunks = [psum.tile([P, PACK, P], F32, name="h_chunk%d" % c, tag="bank") for c in range(BANK // P)]
-        wide = [psum.tile([P, BANK], F32, name="h_wide%d" % t, tag="bank") for t in range(PACK)]
+        def chunk_banks(s):
+            return [psum.tile([P, PACK, P], F32, name="h_chunk%d" % s, tag="bank") for c in range(BANK // P)]
 
-        def chunk_pass(c, a):
+        def chunk_pass(bank, first, a):
             for t in range(PACK):
-                h_pass(
-                    chunks[c][:, t, :], t, a, slice(c * P, (c + 1) * P), a == 0 and t == 0, a == last and t == PACK - 1
-                )
+                h_pass(bank[:, t, :], t, a, slice(first, first + P), a == 0 and t == 0, a == last and t == PACK - 1)
 
+        chunks = [chunk_banks(s) for s in range(EARLY_SLICES)]
         for a in range(last):
-            for c in range(BANK // P):
-                chunk_pass(c, a)
-            for t in range(PACK):
-                h_pass(wide[t][:], t, a, token_cols(1), a == 0, False)
+            for s in range(EARLY_SLICES):
+                for c, bank in enumerate(chunks[s]):
+                    chunk_pass(bank, s * BANK + c * P, a)
 
         def scalar_copy(out, in_):
             nc.scalar.copy(out=out, in_=in_)
@@ -241,35 +237,21 @@ def tile_list_tabres_gelu_kernel(
         h_plane = keep.tile([P, S], U8, name="h_plane", align_bytes=ALIGN)
         for s in range(SLICES):
             cols = token_cols(s)
-            stage_at = (region(1), region(0), results_at(1))[s]
-            grouped = placed(stage_at, [P, BANK * PACK], BF16, "h_bf%d" % s)
-            if s == 0:
-                for c in range(BANK // P):
-                    chunk_pass(c, last)
-                    nc.scalar.copy(
-                        out=grouped[:, c * P * PACK : (c + 1) * P * PACK].rearrange("p (n t) -> p n t", t=PACK),
-                        in_=chunks[c][:].rearrange("p t n -> p n t"),
-                    )
-            else:
-                apart = placed(stage_at + STAGE, [P, PACK, BANK], BF16, "h_apart%d" % s)
-                for t in range(PACK):
-                    if s < EARLY_SLICES:
-                        bank = wide[t]
-                        h_pass(bank[:], t, last, cols, False, True)
-                    else:
-                        bank = psum.tile([P, BANK], F32, name="h_late", tag="bank")
-                        for a in range(PASSES):
-                            h_pass(bank[:], t, a, cols, a == 0, a == last)
-                    nc.scalar.copy(out=apart[:, t, :], in_=bank[:])
-                nc.vector.tensor_copy(
-                    out=grouped[:].rearrange("p (c i t) -> p c t i", i=LINE, t=PACK),
-                    in_=apart[:].rearrange("p t (c i) -> p c t i", i=LINE),
+            grouped = placed(results_at(1) + s * STAGE, [P, BANK * PACK], BF16, "h_bf%d" % s)
+            if s == EARLY_SLICES:
+                chunks.append(chunk_banks(s))
+            for c, bank in enumerate(chunks[s]):
+                for a in range(last if s < EARLY_SLICES else 0, PASSES):
+                    chunk_pass(bank, s * BANK + c * P, a)
+                nc.scalar.copy(
+                    out=grouped[:, c * P * PACK : (c + 1) * P * PACK].rearrange("p (n t) -> p n t", t=PACK),
+                    in_=bank[:].rearrange("p t n -> p n t"),
                 )
             nc.vector.quantize_mx(out=h_codes[:, cols].bitcast(FP8X4), scales=h_plane[:, cols], in_=grouped[:])
             if s == 0:
-                quantise_up(vector_copy, 0, placed(results_at(1) + 2 * STAGE, [P, HALF * PACK], BF16, "up_bf0"))
+                quantise_up(vector_copy, 0, placed(results_at(1) + SLICES * STAGE, [P, HALF * PACK], BF16, "up_bf0"))
 
-        for i in (1, 3, 5):
+        for i in (3, 4, 5):
             load_resid(i)
 
         results = []
@@ -318,11 +300,11 @@ def tile_list_tabres_gelu_kernel(
             if i > 0:
                 nc.vector.tensor_tensor(out=result, in0=resid[i][:].indirect(offsets[:]), in1=act[:], op=ADD)
             if i == 0:
-                load_resid(TILES - 1)
+                load_resid(TILES - 2)
             if i == ACT_BUFS - 1:
                 up_late = acts.tile([P, HALF * PACK], BF16, name="up_bf1", tag="act", align_bytes=ALIGN)
                 quantise_up(scalar_copy, 1, up_late)
-                load_resid(TILES - 2)
+                load_resid(TILES - 1)
             if i == DEAL - 1:
                 store(nc.gpsimd, 0, 0, DEAL)
             if i == TILES - 2:

@@ -70,6 +70,9 @@ def tile_list_tabres_gelu_kernel(
         def entries(s):
             return offsets[:, s * BANK // GROUP : (s + 1) * BANK // GROUP]
 
+        ident = keep.tile([P, P], F32, name="ident")
+        make_identity(nc, ident[:])
+
         down_raw = []
         for a in range(PASSES):
             rows = placed(results_at(1) + a * 4 * PACK * R, [P, PACK * R], F32, "down_raw%d" % a)
@@ -77,9 +80,6 @@ def tile_list_tabres_gelu_kernel(
                 out=rows[:], in_=down[a * K_PASS : (a + 1) * K_PASS, :].rearrange("(p j) r -> p (j r)", j=PACK)
             )
             down_raw.append(rows)
-            if a == 0:
-                ident = keep.tile([P, P], F32, name="ident")
-                make_identity(nc, ident[:])
         table = []
         for a in range(PASSES):
             words = placed(region(a), [P, T], U32, "table%d" % a)
@@ -183,7 +183,7 @@ def tile_list_tabres_gelu_kernel(
         for a in range(PASSES):
             codes = keep.tile([P, S], U32, name="v_codes%d" % a, align_bytes=ALIGN)
             v_codes.append(codes)
-            if a < last:
+            if a == 0:
                 nc.vector.tensor_copy(out=codes[:], in_=table[a][:].indirect(offsets[:]))
             else:
                 for s in range(SLICES):
@@ -243,9 +243,10 @@ def tile_list_tabres_gelu_kernel(
             for c, bank in enumerate(chunks[s]):
                 for a in range(last if s < EARLY_SLICES else 0, PASSES):
                     chunk_pass(bank, s * BANK + c * P, a)
-                nc.scalar.copy(
-                    out=grouped[:, c * P * PACK : (c + 1) * P * PACK].rearrange("p (n t) -> p n t", t=PACK),
-                    in_=bank[:].rearrange("p t n -> p n t"),
+                copy = scalar_copy if s < EARLY_SLICES else vector_copy
+                copy(
+                    grouped[:, c * P * PACK : (c + 1) * P * PACK].rearrange("p (n t) -> p n t", t=PACK),
+                    bank[:].rearrange("p t n -> p n t"),
                 )
             nc.vector.quantize_mx(out=h_codes[:, cols].bitcast(FP8X4), scales=h_plane[:, cols], in_=grouped[:])
             if s == 0:

from contextlib import ExitStack

import concourse.mybir as mybir
from concourse.masks import make_identity

K, M, T, S, R = 1536, 1024, 4096, 1536, 512
FLOPS = 2 * S * (K * M + K * R + R * M)

F32 = mybir.dt.float32
BF16 = mybir.dt.bfloat16
I32 = mybir.dt.int32
U32 = mybir.dt.uint32
U16 = mybir.dt.uint16
U8 = mybir.dt.uint8
FP8X4 = mybir.dt.float8_e4m3fn_x4
FP4X4 = mybir.dt.float4_e2m1fn_x4
ADD = mybir.AluOpType.add
GELU = mybir.ActivationFunctionType.Gelu_apprx_tanh

P = 128
PACK = 4
K_PASS = P * PACK
PASSES = K // K_PASS
BANK = 512
BANKS = 8
SLICES = S // BANK
TILES = M // P
QUAD = 32
PLANE_ROWS = 4
GROUP = 16
DEAL = 4
HALVES = TILES // DEAL
HALF = M // HALVES
BURST = 512
ALIGN = 64
REGION = 4 * T
RESULTS = 4 * DEAL * S
STAGE = 2 * PACK * BANK
REGIONS = 7
UP_REGION = PASSES
RESID_REGIONS = (4, 5, 6, 0, 1, 2, 4, 3)
EARLY_SLICES = BANKS // PACK
ACT_BUFS = 3


def tile_list_tabres_gelu_kernel(
    tc, tab_words, tab_scales, w4_words, w4_scales, down, up, rT, b, offs, out
):
    nc = tc.nc
    with ExitStack() as ctx:
        keep = ctx.enter_context(tc.tile_pool(name="keep", bufs=1))
        big = ctx.enter_context(tc.tile_pool(name="big", bufs=1))
        acts = ctx.enter_context(tc.tile_pool(name="acts", bufs=ACT_BUFS))
        psum = ctx.enter_context(tc.psum_pool(name="psum", bufs=BANKS))

        def placed(offset, shape, dtype, name):
            return big.tile(shape, dtype, name=name, align_bytes=BURST, offset=offset)

        def region(n):
            return n * REGION

        def results_at(g):
            return region(REGIONS) + g * RESULTS

        def token_cols(s):
            return slice(s * BANK, (s + 1) * BANK)

        offsets = keep.tile([P, S // GROUP], U16, name="offsets")

        def entries(s):
            return offsets[:, s * BANK // GROUP : (s + 1) * BANK // GROUP]

        ident = keep.tile([P, P], F32, name="ident")
        make_identity(nc, ident[:])

        down_raw = []
        for a in range(PASSES):
            rows = placed(results_at(1) + a * 4 * PACK * R, [P, PACK * R], F32, "down_raw%d" % a)
            nc.gpsimd.dma_start(
                out=rows[:], in_=down[a * K_PASS : (a + 1) * K_PASS, :].rearrange("(p j) r -> p (j r)", j=PACK)
            )
            down_raw.append(rows)
        table = []
        for a in range(PASSES):
            words = placed(region(a), [P, T], U32, "table%d" % a)
            nc.gpsimd.dma_start(
                out=words[:].bitcast(I32), in_=tab_words[a].rearrange("p t i -> p (t i)").bitcast(I32)
            )
            table.append(words)
        up_raw = placed(region(UP_REGION), [P, PACK, M], F32, "up_raw")
        nc.gpsimd.dma_start(out=up_raw[:], in_=up.rearrange("(p j) n -> p j n", j=PACK))

        resid = {}

        def load_resid(i):
            rows = placed(region(RESID_REGIONS[i]), [P, T], F32, "resid%d" % i)
            g, u = divmod(i, DEAL)
            nc.gpsimd.dma_start(out=rows[:], in_=rT[g * HALF + u : (g + 1) * HALF : DEAL, :])
            resid[i] = rows

        for i in (0, 1, 2):
            load_resid(i)

        window = placed(results_at(0) + PASSES * STAGE + PASSES * 2 * M, [P, T], U8, "window")
        w4_plane_raw = keep.tile([P, PASSES, M], U8, name="w4_plane_raw", align_bytes=BURST)
        v_planes = [keep.tile([P, S], U8, name="v_plane%d" % a, align_bytes=BURST) for a in range(PASSES)]

        def clear(words):
            nc.vector.memset(words[:, :1], 0)
            nc.vector.memset(words[:, 1:], 0)

        clear(window[:].bitcast(I32))
        clear(w4_plane_raw[:].rearrange("p a n -> p (a n)").bitcast(I32))
        for plane in v_planes:
            clear(plane[:].bitcast(I32))

        w4_raw = placed(results_at(0) + PASSES * STAGE, [P, PASSES, 2 * M], U8, "w4_raw")
        nc.sync.dma_start(out=w4_raw[:].bitcast(I32), in_=w4_words.rearrange("a p n -> p a n").bitcast(I32))
        nc.sync.dma_start(offsets[:], offs)
        for c in range(PASSES):
            nc.sync.dma_start(
                out=window[QUAD + c : 3 * QUAD : PLANE_ROWS, :].bitcast(I32), in_=tab_scales[c].bitcast(I32)
            )
        for r in range(PLANE_ROWS):
            nc.sync.dma_start(
                out=w4_plane_raw[r:P:QUAD, :, :].bitcast(I32),
                in_=w4_scales[:, r::PLANE_ROWS, :].rearrange("a q n -> q a n").bitcast(I32),
            )

        b_rows = placed(results_at(1) - 4 * DEAL * P, [P, DEAL * P], F32, "b_rows")
        clear(b_rows[:])
        nc.scalar.dma_start(out=b_rows[GROUP : GROUP + HALVES, :], in_=b.rearrange("(g c) -> g c", g=HALVES))
        b_bank = psum.tile([P, DEAL, P], F32, name="b_bank", tag="bank")
        for u in range(DEAL):
            nc.tensor.transpose(b_bank[:, u, :], b_rows[:, u::DEAL], ident[:])
        bias = keep.tile([P, HALVES, DEAL], F32, name="bias")
        nc.scalar.copy(out=bias[:], in_=b_bank[:, :, GROUP : GROUP + HALVES].rearrange("p u g -> p g u"))

        w4 = []
        for g in range(HALVES):
            words = keep.tile([P, PASSES, 2 * HALF], U8, name="w4_%d" % g, align_bytes=ALIGN)
            nc.scalar.copy(
                out=words[:].bitcast(U16).rearrange("p a (u m) -> p u a m", u=DEAL),
                in_=w4_raw[:].bitcast(U16)[:, :, g * HALF : (g + 1) * HALF].rearrange("p a (m u) -> p u a m", u=DEAL),
            )
            w4.append(words)

        picked = keep.tile([P, S], U8, name="picked", align_bytes=BURST)
        nc.vector.tensor_copy(out=picked[:], in_=window[:].indirect(offsets[:]))
        for a in range(PASSES):
            for r in range(PLANE_ROWS):
                first = QUAD + a + PLANE_ROWS * r
                nc.sync.dma_start(
                    out=v_planes[a][r:P:QUAD, :].bitcast(I32),
                    in_=picked[first : 3 * QUAD : PLANE_ROWS * PLANE_ROWS, :].bitcast(I32),
                )

        w4_plane = []
        for g in range(HALVES):
            plane = keep.tile([P, PASSES, HALF], U8, name="w4_plane%d" % g, align_bytes=ALIGN)
            nc.vector.tensor_copy(
                out=plane[:].rearrange("p a (u m) -> p u a m", u=DEAL),
                in_=w4_plane_raw[:, :, g * HALF : (g + 1) * HALF].rearrange("p a (m u) -> p u a m", u=DEAL),
            )
            w4_plane.append(plane)

        down_codes = []
        down_planes = []
        for a in range(PASSES):
            grouped = placed(results_at(0) + a * STAGE, [P, R * PACK], BF16, "down_bf%d" % a)
            nc.scalar.copy(
                out=grouped[:].rearrange("p (t m j) -> p m t j", t=PACK, j=PACK),
                in_=down_raw[a][:].rearrange("p (j m t) -> p m t j", j=PACK, t=PACK),
            )
            codes = keep.tile([P, R], U32, name="down_codes%d" % a, align_bytes=ALIGN)
            plane = keep.tile([P, R], U8, name="down_plane%d" % a, align_bytes=ALIGN)
            nc.vector.quantize_mx(out=codes[:].bitcast(FP8X4), scales=plane[:], in_=grouped[:])
            down_codes.append(codes)
            down_planes.append(plane)

        last = PASSES - 1
        v_codes = []
        for a in range(PASSES):
            codes = keep.tile([P, S], U32, name="v_codes%d" % a, align_bytes=ALIGN)
            v_codes.append(codes)
            if a == 0:
                nc.vector.tensor_copy(out=codes[:], in_=table[a][:].indirect(offsets[:]))
            else:
                for s in range(SLICES):
                    nc.vector.tensor_copy(out=codes[:, token_cols(s)], in_=table[a][:].indirect(entries(s)))

        def h_pass(sums, t, a, cols, start, stop):
            nc.tensor.matmul_mx(
                out=sums,
                lhsT=down_codes[a][:, t * P : (t + 1) * P].bitcast(FP8X4),
                lhsT_scale=down_planes[a][:, t * P : (t + 1) * P],
                rhs=v_codes[a][:, cols].bitcast(FP8X4),
                rhs_scale=v_planes[a][:, cols],
                start=start,
                stop=stop,
            )

        def chunk_banks(s):
            return [psum.tile([P, PACK, P], F32, name="h_chunk%d" % s, tag="bank") for c in range(BANK // P)]

        def chunk_pass(bank, first, a):
            for t in range(PACK):
                h_pass(bank[:, t, :], t, a, slice(first, first + P), a == 0 and t == 0, a == last and t == PACK - 1)

        chunks = [chunk_banks(s) for s in range(EARLY_SLICES)]
        for a in range(last):
            for s in range(EARLY_SLICES):
                for c, bank in enumerate(chunks[s]):
                    chunk_pass(bank, s * BANK + c * P, a)

        def scalar_copy(out, in_):
            nc.scalar.copy(out=out, in_=in_)

        def vector_copy(out, in_):
            nc.vector.tensor_copy(out=out, in_=in_)

        up_codes = []
        up_planes = []

        def quantise_up(copy, g, grouped):
            copy(
                grouped[:].rearrange("p (u m j) -> p m u j", u=DEAL, j=PACK),
                up_raw[:, :, g * HALF : (g + 1) * HALF].rearrange("p j (m u) -> p m u j", u=DEAL),
            )
            codes = keep.tile([P, HALF], U32, name="up_codes%d" % g, align_bytes=ALIGN)
            plane = keep.tile([P, HALF], U8, name="up_plane%d" % g, align_bytes=ALIGN)
            nc.vector.quantize_mx(out=codes[:].bitcast(FP8X4), scales=plane[:], in_=grouped[:])
            up_codes.append(codes)
            up_planes.append(plane)

        h_codes = keep.tile([P, S], U32, name="h_codes", align_bytes=ALIGN)
        h_plane = keep.tile([P, S], U8, name="h_plane", align_bytes=ALIGN)
        for s in range(SLICES):
            cols = token_cols(s)
            grouped = placed(results_at(1) + s * STAGE, [P, BANK * PACK], BF16, "h_bf%d" % s)
            if s == EARLY_SLICES:
                chunks.append(chunk_banks(s))
            for c, bank in enumerate(chunks[s]):
                for a in range(last if s < EARLY_SLICES else 0, PASSES):
                    chunk_pass(bank, s * BANK + c * P, a)
                copy = scalar_copy if s < EARLY_SLICES else vector_copy
                copy(
                    grouped[:, c * P * PACK : (c + 1) * P * PACK].rearrange("p (n t) -> p n t", t=PACK),
                    bank[:].rearrange("p t n -> p n t"),
                )
            nc.vector.quantize_mx(out=h_codes[:, cols].bitcast(FP8X4), scales=h_plane[:, cols], in_=grouped[:])
            if s == 0:
                quantise_up(vector_copy, 0, placed(results_at(1) + SLICES * STAGE, [P, HALF * PACK], BF16, "up_bf0"))

        for i in (3, 4, 5):
            load_resid(i)

        results = []

        def store(queue, g, first, end):
            dealt = out[g * HALF : (g + 1) * HALF, :].rearrange("(p u) s -> p (u s)", u=DEAL)
            queue.dma_start(
                out=dealt[:, first * S : end * S],
                in_=results[g][:].rearrange("p u s -> p (u s)")[:, first * S : end * S],
            )

        for i in range(TILES):
            g, u = divmod(i, DEAL)
            if u == 0:
                results.append(placed(results_at(g), [P, DEAL, S], F32, "results%d" % g))
            rows = slice(u * P, (u + 1) * P)
            act = acts.tile([P, S], F32, name="act", tag="act", align_bytes=ALIGN)
            result = results[g][:, u, :]
            for s in range(SLICES):
                cols = token_cols(s)
                bank = psum.tile([P, BANK], F32, name="y_bank", tag="bank")
                for a in range(PASSES):
                    nc.tensor.matmul_mx(
                        out=bank[:],
                        lhsT=w4[g][:, a, 2 * u * P : 2 * (u + 1) * P].bitcast(FP4X4),
                        lhsT_scale=w4_plane[g][:, a, rows],
                        rhs=v_codes[a][:, cols].bitcast(FP8X4),
                        rhs_scale=v_planes[a][:, cols],
                        start=(a == 0),
                        stop=False,
                    )
                nc.tensor.matmul_mx(
                    out=bank[:],
                    lhsT=up_codes[g][:, rows].bitcast(FP8X4),
                    lhsT_scale=up_planes[g][:, rows],
                    rhs=h_codes[:, cols].bitcast(FP8X4),
                    rhs_scale=h_plane[:, cols],
                    start=False,
                    stop=True,
                )
                nc.scalar.activation(out=act[:, cols], in_=bank[:], func=GELU, bias=bias[:, g, u : u + 1])
                if i == 0:
                    nc.vector.tensor_tensor(
                        out=result[:, cols], in0=resid[i][:].indirect(entries(s)), in1=act[:, cols], op=ADD
                    )
            if i > 0:
                nc.vector.tensor_tensor(out=result, in0=resid[i][:].indirect(offsets[:]), in1=act[:], op=ADD)
            if i == 0:
                load_resid(TILES - 2)
            if i == ACT_BUFS - 1:
                up_late = acts.tile([P, HALF * PACK], BF16, name="up_bf1", tag="act", align_bytes=ALIGN)
                quantise_up(scalar_copy, 1, up_late)
                load_resid(TILES - 1)
            if i == DEAL - 1:
                store(nc.gpsimd, 0, 0, DEAL)
            if i == TILES - 2:
                store(nc.sync, 1, 0, DEAL - 1)
        store(nc.sync, 1, DEAL - 1, DEAL)
